import numpy as np
import ml_dtypes


def mxq(x, axis, fmt="e4m3"):
    dtype, down = {"e4m3": (ml_dtypes.float8_e4m3fn, 7), "e5m2": (ml_dtypes.float8_e5m2, 14)}[fmt]
    v = np.moveaxis(np.asarray(x, np.float32).astype(ml_dtypes.bfloat16).astype(np.float64), axis, -1)
    blocks = v.reshape(v.shape[:-1] + (-1, 32))
    amax = np.abs(blocks).max(-1, keepdims=True)
    byte = np.maximum(np.where(amax > 0, np.frexp(amax)[1] - 1 + 127, 0) - down, 1)
    scale = np.exp2(byte - 127.0)
    codes = (blocks / scale).astype(np.float32).astype(dtype).astype(np.float64)
    return np.moveaxis((codes * scale).reshape(v.shape), -1, axis)


WIDE = False


def mx_kscale(k):
    if not WIDE:
        return np.ones(k)
    levels = np.array([18, -18])
    if k % 512:
        return np.exp2(np.random.permutation(np.resize(levels, k // 32))).repeat(32)
    a = np.empty((k // 512, 16))
    for p in range(k // 512):
        a[p, :8] = np.random.permutation(np.resize(levels, 8))
        for g in range(8):
            far = levels[np.abs(levels - a[p, g]) >= 10]
            a[p, g + 8] = far[np.random.randint(len(far))]
    return np.exp2(a.ravel()).repeat(32)


def f64(x):
    return np.asarray(x).astype(np.float64)


def striped(idx):
    return np.tile(np.asarray(idx).reshape(-1, 16).T, (8, 1)).astype(np.uint16)


def unstriped(offs):
    return offs[:16].T.reshape(-1).astype(np.int64)


E2M1 = np.array([0.0, 0.5, 1.0, 1.5, 2.0, 3.0, 4.0, 6.0, -0.0, -0.5, -1.0, -1.5, -2.0, -3.0, -4.0, -6.0])


def pack_weight(w, fmt):
    k, n = w.shape
    w = f64(np.asarray(w, np.float32).astype(ml_dtypes.bfloat16)).reshape(k // 32, 32, n)
    amax = np.abs(w).max(1)
    if fmt == "e4m3":
        byte = np.frexp(amax)[1] - 1 + 127 - 7
    else:
        mant, ex = np.frexp(amax / 6.0)
        byte = np.where(mant > 0.5, ex, ex - 1) + 127
    byte = np.clip(np.where(amax > 0, byte, 1), 1, 254)
    scaled = (w * np.exp2(127.0 - byte)[:, None, :]).reshape(k, n).astype(np.float32)
    by_word = np.ascontiguousarray(scaled.reshape(k // 512, 128, 4, n).transpose(0, 1, 3, 2))
    if fmt == "e4m3":
        words = by_word.astype(ml_dtypes.float8_e4m3fn).view(np.uint8)
    else:
        c = by_word.astype(ml_dtypes.float4_e2m1fn).view(np.uint8) & 0xF
        words = (c[..., 0::2] | (c[..., 1::2] << 4)).reshape(k // 512, 128, 2 * n)
    return np.ascontiguousarray(words), np.ascontiguousarray(byte.astype(np.uint8).reshape(k // 512, 16, n))


def unpack_weight(words, scales, fmt):
    g, _, n = scales.shape
    words = np.ascontiguousarray(words).reshape(g, 128, n, -1)
    if fmt == "e4m3":
        vals = words.view(ml_dtypes.float8_e4m3fn).astype(np.float64)
    else:
        nib = np.empty((g, 128, n, 4), np.uint8)
        nib[..., 0::2] = words & 0xF
        nib[..., 1::2] = words >> 4
        vals = E2M1[nib]
    vals = vals * np.repeat(np.exp2(scales.astype(np.float64) - 127.0), 8, axis=1)[..., None]
    return vals.transpose(0, 1, 3, 2).reshape(g * 512, n)


B, N, T, D, R = 1, 512, 2048, 512, 512


def setup_inputs():
    n = np.random.standard_normal
    idx = np.random.permutation(T)[:B * N]
    s = mx_kscale(D)[:, None]
    z = mx_kscale(R)[:, None]
    x = n((B, D, R))
    wp = pack_weight(n((D, T)) * (1.00 / np.sqrt(D)) / s, "e4m3")
    return {
        "xT": (x * s).astype(np.float32),
        "w_words": wp[0],
        "w_scales": wp[1],
        "y": (2 * np.random.randint(0, 2, (B, R, N)) - 1).astype(np.float32),
        "wt": (np.random.uniform(0.5, 1.5, (B, R, 1)) * 1.0 / np.sqrt(R) * z).astype(np.float32),
        "xm": (x.transpose(0, 2, 1) / z).astype(np.float32),
        "offs": striped(idx),
    }


def reference(xT, w_words, w_scales, y, wt, xm, offs):
    idx = unstriped(offs)
    w = unpack_weight(w_words, w_scales, "e4m3")
    pick = lambda x: x[:, idx].reshape(x.shape[0], B, N).transpose(1, 0, 2)
    a = mxq(f64(xT), 1, "e4m3").transpose(0, 2, 1) @ pick(w)
    g = -f64(wt) * f64(y) * np.maximum(1.0 - f64(y) * a, 0.0)
    dw = mxq(f64(xm), 1, "e4m3").transpose(0, 2, 1) @ mxq(g, 1, "e5m2")
    gw = np.zeros((D, T))
    gw[:, idx] = dw.transpose(1, 0, 2).reshape(D, B * N)
    return gw

@@ -1,0 +1,179 @@
+from contextlib import ExitStack
+
+import concourse.mybir as mybir
+
+F32 = mybir.dt.float32
+BF16 = mybir.dt.bfloat16
+I32 = mybir.dt.int32
+U32 = mybir.dt.uint32
+U16 = mybir.dt.uint16
+U8 = mybir.dt.uint8
+E4M3 = mybir.dt.float8_e4m3fn_x4
+E5M2 = mybir.dt.float8_e5m2_x4
+ACT = mybir.ActivationFunctionType
+ALU = mybir.AluOpType
+
+P = 128
+PACK = 4
+N, T, D, R = 512, 2048, 512, 512
+HALF = N // 2
+FLOPS = 2 * 2 * N * D * R
+WINDOWS = 3
+EARLY = 2
+
+
+def tile_attend_gsqh_w_kernel(tc, xT, w_words, w_scales, y, wt, xm, offs, out):
+    nc = tc.nc
+    with ExitStack() as ctx:
+        keep = ctx.enter_context(tc.tile_pool(name="keep", bufs=1))
+        psum = ctx.enter_context(tc.psum_pool(name="psum", bufs=1))
+        psum_dw = ctx.enter_context(tc.psum_pool(name="psum_dw", bufs=4))
+
+        offsets = keep.tile([P, N // 16], U16, name="offsets")
+        half_offsets = [offsets[:, h * HALF // 16 : (h + 1) * HALF // 16] for h in range(2)]
+
+        table_scales = keep.tile([P, T // 4], I32, name="table_scales", align_bytes=64)
+        nc.vector.memset(table_scales[:], 0)
+        scale_rows = w_scales[0].bitcast(I32).rearrange("(q r) n -> r q n", r=4)
+        for r in range(4):
+            nc.scalar.dma_start(out=table_scales[r:P:32, :], in_=scale_rows[r])
+
+        xT_rows = xT[0].rearrange("(p j) r -> p j r", j=PACK)
+        xT_raw = [keep.tile([P, PACK, R // 2], F32, name="xT_raw%d" % h) for h in range(2)]
+        for h in range(2):
+            nc.sync.dma_start(out=xT_raw[h][:], in_=xT_rows[:, :, h * R // 2 : (h + 1) * R // 2])
+        nc.sync.dma_start(offsets[:], offs)
+        table_words = keep.tile([P, T], I32, name="table_words", align_bytes=64)
+        nc.sync.dma_start(out=table_words[:], in_=w_words[0].rearrange("p n j -> p (n j)").bitcast(I32))
+        wt_sb = keep.tile([P, PACK], F32, name="wt_sb")
+        nc.sync.dma_start(out=wt_sb[:], in_=wt[0].rearrange("(p t) o -> p (t o)", t=PACK))
+        y_rows = y[0].rearrange("(p t) n -> p t n", t=PACK)
+        y_sb = [keep.tile([P, 2, N], F32, name="y_sb%d" % u) for u in range(2)]
+        for u in range(2):
+            nc.sync.dma_start(out=y_sb[u][:], in_=y_rows[:, 2 * u : 2 * u + 2, :])
+        xm_rows = xm[0].rearrange("(p j) d -> p j d", j=PACK)
+        xm_raw = [keep.tile([P, PACK, D // 2], F32, name="xm_raw%d" % h) for h in range(2)]
+        for h in range(2):
+            nc.sync.dma_start(out=xm_raw[h][:], in_=xm_rows[:, :, h * D // 2 : (h + 1) * D // 2])
+
+        xT_bf = keep.tile([P, R * PACK], BF16, name="xT_bf", align_bytes=64)
+        xT_bf_by_row = xT_bf[:].rearrange("p (t m j) -> p m j t", t=PACK, j=PACK)
+        for h in range(2):
+            nc.scalar.copy(
+                out=xT_bf_by_row[:, h * P // 2 : (h + 1) * P // 2],
+                in_=xT_raw[h][:].rearrange("p j (m t) -> p m j t", t=PACK),
+            )
+        neg_wt = keep.tile([P, PACK], F32, name="neg_wt")
+        nc.scalar.activation(out=neg_wt[:], in_=wt_sb[:], func=ACT.Copy, scale=-1.0)
+
+        w_scale = keep.tile([P, N], U8, name="w_scale", align_bytes=64)
+        nc.vector.tensor_copy(w_scale[:], table_scales[:].bitcast(U8).indirect(offsets[:]))
+        xT_codes = keep.tile([P, R], U32, name="xT_codes", align_bytes=64)
+        xT_scale = keep.tile([P, R], U8, name="xT_scale", align_bytes=64)
+        nc.vector.quantize_mx(out=xT_codes[:].bitcast(E4M3), scales=xT_scale[:], in_=xT_bf[:])
+
+        g_codes = keep.tile([P, HALF + N], I32, name="g_codes", align_bytes=64)
+        g_scale = keep.tile([P, HALF + N], U8, name="g_scale", align_bytes=64)
+        nc.vector.memset(g_codes[:, 0:HALF], 0)
+        nc.vector.memset(g_scale[:, 0:HALF].bitcast(I32), 0)
+        windows = [keep.tile([P, T], F32, name="window%d" % k) for k in range(WINDOWS)]
+        for window in windows:
+            nc.vector.memset(window[:], 0.0)
+
+        w_codes = [keep.tile([P, HALF], U32, name="w_codes%d" % h, align_bytes=64) for h in range(2)]
+        scores = {}
+        for h in range(2):
+            nc.vector.tensor_copy(w_codes[h][:], table_words[:].bitcast(U32).indirect(half_offsets[h]))
+            for u in range(2):
+                scores[h, u] = psum.tile([P, 2, HALF], F32, name="scores%d%d" % (h, u))
+                for e in range(2):
+                    t = 2 * u + e
+                    nc.tensor.matmul_mx(
+                        out=scores[h, u][:, e, :],
+                        lhsT=xT_codes[:, t * P : (t + 1) * P].bitcast(E4M3),
+                        lhsT_scale=xT_scale[:, t * P : (t + 1) * P],
+                        rhs=w_codes[h][:].bitcast(E4M3),
+                        rhs_scale=w_scale[:, h * HALF : (h + 1) * HALF],
+                        start=True,
+                        stop=True,
+                    )
+
+        factor = keep.tile([P, PACK, N], F32, name="factor")
+        for t in range(PACK):
+            nc.gpsimd.tensor_scalar(
+                out=factor[:, t, :], in0=y_sb[t // 2][:, t % 2, :], scalar1=neg_wt[:, t : t + 1], scalar2=0.0,
+                op0=ALU.mult, op1=ALU.add,
+            )
+        margin = [keep.tile([P, PACK, HALF], F32, name="margin%d" % h) for h in range(2)]
+        hinge = [keep.tile([P, PACK, HALF], F32, name="hinge%d" % h) for h in range(2)]
+        for u in range(2):
+            for h in range(2):
+                nc.vector.tensor_tensor(
+                    out=margin[h][:, 2 * u : 2 * u + 2, :], in0=scores[h, u][:],
+                    in1=y_sb[u][:, :, h * HALF : (h + 1) * HALF], op=ALU.mult,
+                )
+                nc.scalar.activation(
+                    out=hinge[h][:, 2 * u : 2 * u + 2, :], in_=margin[h][:, 2 * u : 2 * u + 2, :],
+                    func=ACT.Relu, bias=1.0, scale=-1.0,
+                )
+
+        xm_bf = [keep.tile([P, P * PACK], BF16, name="xm_bf%d" % k, align_bytes=64) for k in range(D // P)]
+        xm_codes = [keep.tile([P, P], U32, name="xm_codes%d" % k, align_bytes=64) for k in range(D // P)]
+        xm_scale = [keep.tile([P, P], U8, name="xm_scale%d" % k, align_bytes=64) for k in range(D // P)]
+
+        def round_xm(k):
+            nc.scalar.copy(
+                out=xm_bf[k][:].rearrange("p (c i j) -> p c j i", i=4, j=PACK),
+                in_=xm_raw[k // 2][:, :, (k % 2) * P : (k % 2 + 1) * P].rearrange("p j (c i) -> p c j i", i=4),
+            )
+
+        def quantize_xm(k):
+            nc.vector.quantize_mx(out=xm_codes[k][:].bitcast(E4M3), scales=xm_scale[k][:], in_=xm_bf[k][:])
+
+        g_bf = [keep.tile([P, HALF * PACK], BF16, name="g_bf%d" % h, align_bytes=64) for h in range(2)]
+
+        def make_g(h):
+            nc.vector.tensor_tensor(
+                out=g_bf[h][:].rearrange("p (c i t) -> p c t i", i=4, t=PACK),
+                in0=hinge[h][:].rearrange("p t (c i) -> p c t i", i=4),
+                in1=factor[:, :, h * HALF : (h + 1) * HALF].rearrange("p t (c i) -> p c t i", i=4),
+                op=ALU.mult,
+            )
+
+        def quantize_g(h):
+            cols = slice((h + 1) * HALF, (h + 2) * HALF)
+            nc.vector.quantize_mx(out=g_codes[:, cols].bitcast(E5M2), scales=g_scale[:, cols], in_=g_bf[h][:])
+
+        def gradient(k, first, keep_from, name):
+            acc = psum_dw.tile([P, N], F32, name="acc")
+            nc.tensor.matmul_mx(
+                out=acc[:],
+                lhsT=xm_codes[k][:].bitcast(E4M3),
+                lhsT_scale=xm_scale[k][:],
+                rhs=g_codes[:, first : first + N].bitcast(E5M2),
+                rhs_scale=g_scale[:, first : first + N],
+                start=True,
+                stop=True,
+            )
+            dw = keep.tile([P, N - keep_from], F32, name=name)
+            nc.scalar.copy(out=dw[:], in_=acc[:, keep_from:N])
+            return dw
+
+        for k in range(D // P):
+            round_xm(k)
+        make_g(0)
+        quantize_xm(0)
+        quantize_g(0)
+        quantize_xm(1)
+        early = [gradient(k, 0, HALF, "dw_early%d" % k) for k in range(EARLY)]
+        make_g(1)
+        quantize_xm(2)
+        quantize_g(1)
+        quantize_xm(3)
+        late = [gradient(k, HALF, HALF if k < EARLY else 0, "dw_late%d" % k) for k in range(D // P)]
+        for k in range(EARLY):
+            nc.vector.tensor_copy(windows[k][:].indirect(half_offsets[0]), early[k][:])
+        for k in range(D // P):
+            window = windows[k % WINDOWS]
+            nc.vector.tensor_copy(window[:].indirect(half_offsets[1] if k < EARLY else offsets[:]), late[k][:])
+            nc.sync.dma_start(out=out[k * P : (k + 1) * P, :], in_=window[:])

@@ -33,30 +33,29 @@ def tile_attend_gsqh_w_kernel(tc, xT, w_words, w_scales, y, wt, xm, offs, out):
         half_offsets = [offsets[:, h * HALF // 16 : (h + 1) * HALF // 16] for h in range(2)]
 
         table_scales = keep.tile([P, T // 4], I32, name="table_scales", align_bytes=64)
-        nc.vector.memset(table_scales[:], 0)
+        nc.gpsimd.memset(table_scales[:], 0)
+        g_codes = keep.tile([P, HALF + N], I32, name="g_codes", align_bytes=64)
+        g_scale = keep.tile([P, HALF + N], U8, name="g_scale", align_bytes=64)
+        nc.gpsimd.memset(g_codes[:, 0:HALF], 0)
+        nc.gpsimd.memset(g_scale[:, 0:HALF].bitcast(I32), 0)
+        windows = [keep.tile([P, T], F32, name="window%d" % k) for k in range(WINDOWS)]
+        for window in windows:
+            nc.vector.memset(window[:], 0.0)
+
+        nc.sync.dma_start(offsets[:], offs)
         scale_rows = w_scales[0].bitcast(I32).rearrange("(q r) n -> r q n", r=4)
         for r in range(4):
             nc.scalar.dma_start(out=table_scales[r:P:32, :], in_=scale_rows[r])
-
         xT_rows = xT[0].rearrange("(p j) r -> p j r", j=PACK)
-        xT_raw = [keep.tile([P, PACK, R // 2], F32, name="xT_raw%d" % h) for h in range(2)]
+        xT_raw = [keep.tile([P, PACK, R // 2], F32, name="xT_raw%d" % h, tag="stage%d" % h, align_bytes=64) for h in range(2)]
         for h in range(2):
             nc.sync.dma_start(out=xT_raw[h][:], in_=xT_rows[:, :, h * R // 2 : (h + 1) * R // 2])
-        nc.sync.dma_start(offsets[:], offs)
-        table_words = keep.tile([P, T], I32, name="table_words", align_bytes=64)
-        nc.sync.dma_start(out=table_words[:], in_=w_words[0].rearrange("p n j -> p (n j)").bitcast(I32))
         wt_sb = keep.tile([P, PACK], F32, name="wt_sb")
         nc.sync.dma_start(out=wt_sb[:], in_=wt[0].rearrange("(p t) o -> p (t o)", t=PACK))
-        y_rows = y[0].rearrange("(p t) n -> p t n", t=PACK)
-        y_sb = [keep.tile([P, 2, N], F32, name="y_sb%d" % u) for u in range(2)]
-        for u in range(2):
-            nc.sync.dma_start(out=y_sb[u][:], in_=y_rows[:, 2 * u : 2 * u + 2, :])
-        xm_rows = xm[0].rearrange("(p j) d -> p j d", j=PACK)
-        xm_raw = [keep.tile([P, PACK, D // 2], F32, name="xm_raw%d" % h) for h in range(2)]
-        for h in range(2):
-            nc.sync.dma_start(out=xm_raw[h][:], in_=xm_rows[:, :, h * D // 2 : (h + 1) * D // 2])
+        table_words = keep.tile([P, T], I32, name="table_words", tag="stage2", align_bytes=64)
+        nc.sync.dma_start(out=table_words[:], in_=w_words[0].rearrange("p n j -> p (n j)").bitcast(I32))
 
-        xT_bf = keep.tile([P, R * PACK], BF16, name="xT_bf", align_bytes=64)
+        xT_bf = keep.tile([P, R * PACK], BF16, name="xT_bf", tag="stage3", align_bytes=64)
         xT_bf_by_row = xT_bf[:].rearrange("p (t m j) -> p m j t", t=PACK, j=PACK)
         for h in range(2):
             nc.scalar.copy(
@@ -72,19 +71,17 @@ def tile_attend_gsqh_w_kernel(tc, xT, w_words, w_scales, y, wt, xm, offs, out):
         xT_scale = keep.tile([P, R], U8, name="xT_scale", align_bytes=64)
         nc.vector.quantize_mx(out=xT_codes[:].bitcast(E4M3), scales=xT_scale[:], in_=xT_bf[:])
 
-        g_codes = keep.tile([P, HALF + N], I32, name="g_codes", align_bytes=64)
-        g_scale = keep.tile([P, HALF + N], U8, name="g_scale", align_bytes=64)
-        nc.vector.memset(g_codes[:, 0:HALF], 0)
-        nc.vector.memset(g_scale[:, 0:HALF].bitcast(I32), 0)
-        windows = [keep.tile([P, T], F32, name="window%d" % k) for k in range(WINDOWS)]
-        for window in windows:
-            nc.vector.memset(window[:], 0.0)
+        y_rows = y[0].rearrange("(p t) n -> p t n", t=PACK)
+        y_sb = [keep.tile([P, 2, N], F32, name="y_sb%d" % u, tag="stage%d" % u, align_bytes=64) for u in range(2)]
+        for u in range(2):
+            nc.sync.dma_start(out=y_sb[u][:], in_=y_rows[:, 2 * u : 2 * u + 2, :])
 
         w_codes = [keep.tile([P, HALF], U32, name="w_codes%d" % h, align_bytes=64) for h in range(2)]
         scores = {}
         for h in range(2):
             nc.vector.tensor_copy(w_codes[h][:], table_words[:].bitcast(U32).indirect(half_offsets[h]))
-            for u in range(2):
+        for u in range(2):
+            for h in range(2):
                 scores[h, u] = psum.tile([P, 2, HALF], F32, name="scores%d%d" % (h, u))
                 for e in range(2):
                     t = 2 * u + e
@@ -104,35 +101,49 @@ def tile_attend_gsqh_w_kernel(tc, xT, w_words, w_scales, y, wt, xm, offs, out):
                 out=factor[:, t, :], in0=y_sb[t // 2][:, t % 2, :], scalar1=neg_wt[:, t : t + 1], scalar2=0.0,
                 op0=ALU.mult, op1=ALU.add,
             )
-        margin = [keep.tile([P, PACK, HALF], F32, name="margin%d" % h) for h in range(2)]
-        hinge = [keep.tile([P, PACK, HALF], F32, name="hinge%d" % h) for h in range(2)]
+        hinge = [keep.tile([P, PACK, HALF], F32, name="hinge%d" % h, align_bytes=64) for h in range(2)]
         for u in range(2):
             for h in range(2):
+                margin = keep.tile([P, 2, HALF], F32, name="margin", tag="margin%d%d" % (h, u), align_bytes=64)
                 nc.vector.tensor_tensor(
-                    out=margin[h][:, 2 * u : 2 * u + 2, :], in0=scores[h, u][:],
-                    in1=y_sb[u][:, :, h * HALF : (h + 1) * HALF], op=ALU.mult,
+                    out=margin[:], in0=scores[h, u][:], in1=y_sb[u][:, :, h * HALF : (h + 1) * HALF], op=ALU.mult
                 )
                 nc.scalar.activation(
-                    out=hinge[h][:, 2 * u : 2 * u + 2, :], in_=margin[h][:, 2 * u : 2 * u + 2, :],
-                    func=ACT.Relu, bias=1.0, scale=-1.0,
+                    out=hinge[h][:, 2 * u : 2 * u + 2, :], in_=margin[:], func=ACT.Relu, bias=1.0, scale=-1.0
                 )
 
-        xm_bf = [keep.tile([P, P * PACK], BF16, name="xm_bf%d" % k, align_bytes=64) for k in range(D // P)]
-        xm_codes = [keep.tile([P, P], U32, name="xm_codes%d" % k, align_bytes=64) for k in range(D // P)]
+        xm_rows = xm[0].rearrange("(p j) d -> p j d", j=PACK)
+        xm_raw = [
+            keep.tile([P, PACK, D // 2], F32, name="xm_raw%d" % h, tag=tag, align_bytes=64)
+            for h, tag in enumerate(("stage3", "stage2"))
+        ]
+        for h in range(2):
+            nc.sync.dma_start(out=xm_raw[h][:], in_=xm_rows[:, :, h * D // 2 : (h + 1) * D // 2])
+        xm_bf_tags = ("margin11", "hinge1")
+        xm_bf = {}
+        xm_codes = {}
+        xm_codes_tags = ("hinge0", "xm_codes")
         xm_scale = [keep.tile([P, P], U8, name="xm_scale%d" % k, align_bytes=64) for k in range(D // P)]
 
         def round_xm(k):
+            if k % 2 == 0:
+                pair = keep.tile([P, 2, P * PACK], BF16, name="xm_bf", tag=xm_bf_tags[k // 2], align_bytes=64)
+                xm_bf[k], xm_bf[k + 1] = pair[:, 0, :], pair[:, 1, :]
             nc.scalar.copy(
-                out=xm_bf[k][:].rearrange("p (c i j) -> p c j i", i=4, j=PACK),
+                out=xm_bf[k].rearrange("p (c i j) -> p c j i", i=4, j=PACK),
                 in_=xm_raw[k // 2][:, :, (k % 2) * P : (k % 2 + 1) * P].rearrange("p j (c i) -> p c j i", i=4),
             )
 
         def quantize_xm(k):
-            nc.vector.quantize_mx(out=xm_codes[k][:].bitcast(E4M3), scales=xm_scale[k][:], in_=xm_bf[k][:])
+            if k % 2 == 0:
+                pair = keep.tile([P, 2, P], U32, name="xm_codes", tag=xm_codes_tags[k // 2], align_bytes=64)
+                xm_codes[k], xm_codes[k + 1] = pair[:, 0, :], pair[:, 1, :]
+            nc.vector.quantize_mx(out=xm_codes[k].bitcast(E4M3), scales=xm_scale[k][:], in_=xm_bf[k])
 
-        g_bf = [keep.tile([P, HALF * PACK], BF16, name="g_bf%d" % h, align_bytes=64) for h in range(2)]
+        g_bf = {}
 
         def make_g(h):
+            g_bf[h] = keep.tile([P, HALF * PACK], BF16, name="g_bf", align_bytes=64)
             nc.vector.tensor_tensor(
                 out=g_bf[h][:].rearrange("p (c i t) -> p c t i", i=4, t=PACK),
                 in0=hinge[h][:].rearrange("p t (c i) -> p c t i", i=4),
@@ -148,7 +159,7 @@ def tile_attend_gsqh_w_kernel(tc, xT, w_words, w_scales, y, wt, xm, offs, out):
             acc = psum_dw.tile([P, N], F32, name="acc")
             nc.tensor.matmul_mx(
                 out=acc[:],
-                lhsT=xm_codes[k][:].bitcast(E4M3),
+                lhsT=xm_codes[k].bitcast(E4M3),
                 lhsT_scale=xm_scale[k][:],
                 rhs=g_codes[:, first : first + N].bitcast(E5M2),
                 rhs_scale=g_scale[:, first : first + N],
@@ -159,20 +170,23 @@ def tile_attend_gsqh_w_kernel(tc, xT, w_words, w_scales, y, wt, xm, offs, out):
             nc.scalar.copy(out=dw[:], in_=acc[:, keep_from:N])
             return dw
 
-        for k in range(D // P):
-            round_xm(k)
+        round_xm(0)
+        round_xm(1)
         make_g(0)
         quantize_xm(0)
         quantize_g(0)
+        make_g(1)
         quantize_xm(1)
         early = [gradient(k, 0, HALF, "dw_early%d" % k) for k in range(EARLY)]
-        make_g(1)
-        quantize_xm(2)
         quantize_g(1)
-        quantize_xm(3)
-        late = [gradient(k, HALF, HALF if k < EARLY else 0, "dw_late%d" % k) for k in range(D // P)]
-        for k in range(EARLY):
-            nc.vector.tensor_copy(windows[k][:].indirect(half_offsets[0]), early[k][:])
+        round_xm(2)
+        round_xm(3)
+        late = [gradient(k, HALF, HALF, "dw_late%d" % k) for k in range(EARLY)]
+        nc.vector.tensor_copy(windows[0][:].indirect(half_offsets[0]), early[0][:])
+        for k in range(EARLY, D // P):
+            quantize_xm(k)
+            late.append(gradient(k, HALF, 0, "dw_late%d" % k))
+        nc.vector.tensor_copy(windows[1][:].indirect(half_offsets[0]), early[1][:])
         for k in range(D // P):
             window = windows[k % WINDOWS]
             nc.vector.tensor_copy(window[:].indirect(half_offsets[1] if k < EARLY else offsets[:]), late[k][:])

@@ -101,7 +101,7 @@ def tile_attend_gsqh_w_kernel(tc, xT, w_words, w_scales, y, wt, xm, offs, out):
                 out=factor[:, t, :], in0=y_sb[t // 2][:, t % 2, :], scalar1=neg_wt[:, t : t + 1], scalar2=0.0,
                 op0=ALU.mult, op1=ALU.add,
             )
-        hinge = [keep.tile([P, PACK, HALF], F32, name="hinge%d" % h, align_bytes=64) for h in range(2)]
+        hinge = [keep.tile([P, PACK, HALF], F32, name="hinge%d" % h, tag="hinge%d" % h, align_bytes=64) for h in range(2)]
         for u in range(2):
             for h in range(2):
                 margin = keep.tile([P, 2, HALF], F32, name="margin", tag="margin%d%d" % (h, u), align_bytes=64)
@@ -186,8 +186,11 @@ def tile_attend_gsqh_w_kernel(tc, xT, w_words, w_scales, y, wt, xm, offs, out):
         for k in range(EARLY, D // P):
             quantize_xm(k)
             late.append(gradient(k, HALF, 0, "dw_late%d" % k))
+        last_window = keep.tile([P, T], F32, name="window3", tag="hinge1", align_bytes=64)
+        nc.gpsimd.memset(last_window[:], 0.0)
+        windows.append(last_window)
         nc.vector.tensor_copy(windows[1][:].indirect(half_offsets[0]), early[1][:])
         for k in range(D // P):
-            window = windows[k % WINDOWS]
+            window = windows[k]
             nc.vector.tensor_copy(window[:].indirect(half_offsets[1] if k < EARLY else offsets[:]), late[k][:])
             nc.sync.dma_start(out=out[k * P : (k + 1) * P, :], in_=window[:])

@@ -18,7 +18,6 @@ PACK = 4
 N, T, D, R = 512, 2048, 512, 512
 HALF = N // 2
 FLOPS = 2 * 2 * N * D * R
-WINDOWS = 3
 EARLY = 2
 
 
@@ -33,37 +32,32 @@ def tile_attend_gsqh_w_kernel(tc, xT, w_words, w_scales, y, wt, xm, offs, out):
         half_offsets = [offsets[:, h * HALF // 16 : (h + 1) * HALF // 16] for h in range(2)]
 
         table_scales = keep.tile([P, T // 4], I32, name="table_scales", align_bytes=64)
-        nc.gpsimd.memset(table_scales[:], 0)
-        g_codes = keep.tile([P, HALF + N], I32, name="g_codes", align_bytes=64)
-        g_scale = keep.tile([P, HALF + N], U8, name="g_scale", align_bytes=64)
-        nc.gpsimd.memset(g_codes[:, 0:HALF], 0)
-        nc.gpsimd.memset(g_scale[:, 0:HALF].bitcast(I32), 0)
-        windows = [keep.tile([P, T], F32, name="window%d" % k) for k in range(WINDOWS)]
+        nc.vector.memset(table_scales[:], 0)
+        windows = [keep.tile([P, T], F32, name="window%d" % k) for k in range(EARLY)]
         for window in windows:
             nc.vector.memset(window[:], 0.0)
+        g_codes = keep.tile([P, HALF + N], I32, name="g_codes", align_bytes=64)
+        g_scale = keep.tile([P, HALF + N], U8, name="g_scale", align_bytes=64)
+        nc.vector.memset(g_codes[:, 0:HALF], 0)
+        nc.vector.memset(g_scale[:, 0:HALF].bitcast(I32), 0)
 
         nc.sync.dma_start(offsets[:], offs)
         scale_rows = w_scales[0].bitcast(I32).rearrange("(q r) n -> r q n", r=4)
         for r in range(4):
             nc.scalar.dma_start(out=table_scales[r:P:32, :], in_=scale_rows[r])
-        xT_rows = xT[0].rearrange("(p j) r -> p j r", j=PACK)
-        xT_raw = [keep.tile([P, PACK, R // 2], F32, name="xT_raw%d" % h, tag="stage%d" % h, align_bytes=64) for h in range(2)]
-        for h in range(2):
-            nc.sync.dma_start(out=xT_raw[h][:], in_=xT_rows[:, :, h * R // 2 : (h + 1) * R // 2])
-        wt_sb = keep.tile([P, PACK], F32, name="wt_sb")
-        nc.sync.dma_start(out=wt_sb[:], in_=wt[0].rearrange("(p t) o -> p (t o)", t=PACK))
+        xT_raw = keep.tile([P, PACK, R], F32, name="xT_raw", tag="stage0", align_bytes=64)
+        nc.sync.dma_start(out=xT_raw[:], in_=xT[0].rearrange("(p j) r -> p j r", j=PACK))
         table_words = keep.tile([P, T], I32, name="table_words", tag="stage2", align_bytes=64)
         nc.sync.dma_start(out=table_words[:], in_=w_words[0].rearrange("p n j -> p (n j)").bitcast(I32))
+        y_rows = y[0].rearrange("(p t) n -> p t n", t=PACK)
+        y_first = keep.tile([P, 2, N], F32, name="y_first", align_bytes=64)
+        nc.sync.dma_start(out=y_first[:], in_=y_rows[:, 0:2, :])
 
         xT_bf = keep.tile([P, R * PACK], BF16, name="xT_bf", tag="stage3", align_bytes=64)
         xT_bf_by_row = xT_bf[:].rearrange("p (t m j) -> p m j t", t=PACK, j=PACK)
-        for h in range(2):
-            nc.scalar.copy(
-                out=xT_bf_by_row[:, h * P // 2 : (h + 1) * P // 2],
-                in_=xT_raw[h][:].rearrange("p j (m t) -> p m j t", t=PACK),
-            )
-        neg_wt = keep.tile([P, PACK], F32, name="neg_wt")
-        nc.scalar.activation(out=neg_wt[:], in_=wt_sb[:], func=ACT.Copy, scale=-1.0)
+        xT_raw_by_row = xT_raw[:].rearrange("p j (m t) -> p m j t", t=PACK)
+        nc.vector.tensor_copy(out=xT_bf_by_row[:, 0 : P // 2], in_=xT_raw_by_row[:, 0 : P // 2])
+        nc.scalar.copy(out=xT_bf_by_row[:, P // 2 : P], in_=xT_raw_by_row[:, P // 2 : P])
 
         w_scale = keep.tile([P, N], U8, name="w_scale", align_bytes=64)
         nc.vector.tensor_copy(w_scale[:], table_scales[:].bitcast(U8).indirect(offsets[:]))
@@ -71,10 +65,13 @@ def tile_attend_gsqh_w_kernel(tc, xT, w_words, w_scales, y, wt, xm, offs, out):
         xT_scale = keep.tile([P, R], U8, name="xT_scale", align_bytes=64)
         nc.vector.quantize_mx(out=xT_codes[:].bitcast(E4M3), scales=xT_scale[:], in_=xT_bf[:])
 
-        y_rows = y[0].rearrange("(p t) n -> p t n", t=PACK)
-        y_sb = [keep.tile([P, 2, N], F32, name="y_sb%d" % u, tag="stage%d" % u, align_bytes=64) for u in range(2)]
-        for u in range(2):
-            nc.sync.dma_start(out=y_sb[u][:], in_=y_rows[:, 2 * u : 2 * u + 2, :])
+        y_and_wt = keep.tile([P, 2 * N + 8], F32, name="y_and_wt", tag="stage0", align_bytes=64)
+        wt_sb = y_and_wt[:, 2 * N : 2 * N + PACK]
+        nc.sync.dma_start(out=wt_sb, in_=wt[0].rearrange("(p t) o -> p (t o)", t=PACK))
+        y_sb = [y_first[:], y_and_wt[:, 0 : 2 * N].rearrange("p (t n) -> p t n", t=2)]
+        nc.sync.dma_start(out=y_sb[1], in_=y_rows[:, 2:4, :])
+        neg_wt = keep.tile([P, PACK], F32, name="neg_wt")
+        nc.gpsimd.tensor_scalar(out=neg_wt[:], in0=wt_sb, scalar1=-1.0, scalar2=0.0, op0=ALU.mult, op1=ALU.add)
 
         w_codes = [keep.tile([P, HALF], U32, name="w_codes%d" % h, align_bytes=64) for h in range(2)]
         scores = {}
@@ -166,7 +163,7 @@ def tile_attend_gsqh_w_kernel(tc, xT, w_words, w_scales, y, wt, xm, offs, out):
                 start=True,
                 stop=True,
             )
-            dw = keep.tile([P, N - keep_from], F32, name=name)
+            dw = keep.tile([P, N - keep_from], F32, name=name, tag=name, align_bytes=64)
             nc.scalar.copy(out=dw[:], in_=acc[:, keep_from:N])
             return dw
 
@@ -186,10 +183,11 @@ def tile_attend_gsqh_w_kernel(tc, xT, w_words, w_scales, y, wt, xm, offs, out):
         for k in range(EARLY, D // P):
             quantize_xm(k)
             late.append(gradient(k, HALF, 0, "dw_late%d" % k))
-        last_window = keep.tile([P, T], F32, name="window3", tag="hinge1", align_bytes=64)
-        nc.gpsimd.memset(last_window[:], 0.0)
-        windows.append(last_window)
         nc.vector.tensor_copy(windows[1][:].indirect(half_offsets[0]), early[1][:])
+        for k, tag in ((2, "hinge1"), (3, "dw_early1")):
+            window = keep.tile([P, T], F32, name="window%d" % k, tag=tag, align_bytes=64)
+            nc.gpsimd.memset(window[:], 0.0)
+            windows.append(window)
         for k in range(D // P):
             window = windows[k]
             nc.vector.tensor_copy(window[:].indirect(half_offsets[1] if k < EARLY else offsets[:]), late[k][:])

@@ -19,12 +19,14 @@ N, T, D, R = 512, 2048, 512, 512
 HALF = N // 2
 FLOPS = 2 * 2 * N * D * R
 EARLY = 2
+SPLIT = 48
 
 
 def tile_attend_gsqh_w_kernel(tc, xT, w_words, w_scales, y, wt, xm, offs, out):
     nc = tc.nc
     with ExitStack() as ctx:
         keep = ctx.enter_context(tc.tile_pool(name="keep", bufs=1))
+        shared = ctx.enter_context(tc.tile_pool(name="shared", bufs=1))
         psum = ctx.enter_context(tc.psum_pool(name="psum", bufs=1))
         psum_dw = ctx.enter_context(tc.psum_pool(name="psum_dw", bufs=4))
 
@@ -41,23 +43,34 @@ def tile_attend_gsqh_w_kernel(tc, xT, w_words, w_scales, y, wt, xm, offs, out):
         nc.vector.memset(g_codes[:, 0:HALF], 0)
         nc.vector.memset(g_scale[:, 0:HALF].bitcast(I32), 0)
 
-        nc.sync.dma_start(offsets[:], offs)
-        scale_rows = w_scales[0].bitcast(I32).rearrange("(q r) n -> r q n", r=4)
-        for r in range(4):
-            nc.scalar.dma_start(out=table_scales[r:P:32, :], in_=scale_rows[r])
-        xT_raw = keep.tile([P, PACK, R], F32, name="xT_raw", tag="stage0", align_bytes=64)
+        scale_rows = w_scales[0].bitcast(I32)
+        staged_scales = keep.tile([P, T // 4], I32, name="staged_scales", align_bytes=64)
+        for q in range(4):
+            nc.sync.dma_start(out=staged_scales[32 * q : 32 * q + 4, :], in_=scale_rows[4 * q : 4 * q + 4, :])
+        xT_raw = keep.tile([P, PACK, R], F32, name="xT_raw", align_bytes=64)
         nc.sync.dma_start(out=xT_raw[:], in_=xT[0].rearrange("(p j) r -> p j r", j=PACK))
-        table_words = keep.tile([P, T], I32, name="table_words", tag="stage2", align_bytes=64)
+        nc.sync.dma_start(offsets[:], offs)
+        table_words = keep.tile([P, T], I32, name="table_words", align_bytes=64)
         nc.sync.dma_start(out=table_words[:], in_=w_words[0].rearrange("p n j -> p (n j)").bitcast(I32))
+        wt_sb = keep.tile([P, PACK], F32, name="wt_sb")
+        nc.sync.dma_start(out=wt_sb[:], in_=wt[0].rearrange("(p t) o -> p (t o)", t=PACK))
         y_rows = y[0].rearrange("(p t) n -> p t n", t=PACK)
-        y_first = keep.tile([P, 2, N], F32, name="y_first", align_bytes=64)
-        nc.sync.dma_start(out=y_first[:], in_=y_rows[:, 0:2, :])
+        y_sb = [keep.tile([P, 2, N], F32, name="y_sb%d" % u, align_bytes=64) for u in range(2)]
+        for u in range(2):
+            nc.sync.dma_start(out=y_sb[u][:], in_=y_rows[:, 2 * u : 2 * u + 2, :])
+        xm_rows = xm[0].rearrange("(p j) d -> p j d", j=PACK)
+        xm_raw = [keep.tile([P, PACK, D // 2], F32, name="xm_raw%d" % h, align_bytes=64) for h in range(2)]
+        for h in range(2):
+            nc.sync.dma_start(out=xm_raw[h][:], in_=xm_rows[:, :, h * D // 2 : (h + 1) * D // 2])
 
-        xT_bf = keep.tile([P, R * PACK], BF16, name="xT_bf", tag="stage3", align_bytes=64)
+        for q in range(4):
+            nc.vector.tensor_copy(table_scales[32 * q : 32 * q + 4, :], staged_scales[32 * q : 32 * q + 4, :])
+
+        xT_bf = keep.tile([P, R * PACK], BF16, name="xT_bf", align_bytes=64)
         xT_bf_by_row = xT_bf[:].rearrange("p (t m j) -> p m j t", t=PACK, j=PACK)
         xT_raw_by_row = xT_raw[:].rearrange("p j (m t) -> p m j t", t=PACK)
-        nc.vector.tensor_copy(out=xT_bf_by_row[:, 0 : P // 2], in_=xT_raw_by_row[:, 0 : P // 2])
-        nc.scalar.copy(out=xT_bf_by_row[:, P // 2 : P], in_=xT_raw_by_row[:, P // 2 : P])
+        nc.vector.tensor_copy(out=xT_bf_by_row[:, 0:SPLIT], in_=xT_raw_by_row[:, 0:SPLIT])
+        nc.scalar.copy(out=xT_bf_by_row[:, SPLIT:P], in_=xT_raw_by_row[:, SPLIT:P])
 
         w_scale = keep.tile([P, N], U8, name="w_scale", align_bytes=64)
         nc.vector.tensor_copy(w_scale[:], table_scales[:].bitcast(U8).indirect(offsets[:]))
@@ -65,13 +78,8 @@ def tile_attend_gsqh_w_kernel(tc, xT, w_words, w_scales, y, wt, xm, offs, out):
         xT_scale = keep.tile([P, R], U8, name="xT_scale", align_bytes=64)
         nc.vector.quantize_mx(out=xT_codes[:].bitcast(E4M3), scales=xT_scale[:], in_=xT_bf[:])
 
-        y_and_wt = keep.tile([P, 2 * N + 8], F32, name="y_and_wt", tag="stage0", align_bytes=64)
-        wt_sb = y_and_wt[:, 2 * N : 2 * N + PACK]
-        nc.sync.dma_start(out=wt_sb, in_=wt[0].rearrange("(p t) o -> p (t o)", t=PACK))
-        y_sb = [y_first[:], y_and_wt[:, 0 : 2 * N].rearrange("p (t n) -> p t n", t=2)]
-        nc.sync.dma_start(out=y_sb[1], in_=y_rows[:, 2:4, :])
         neg_wt = keep.tile([P, PACK], F32, name="neg_wt")
-        nc.gpsimd.tensor_scalar(out=neg_wt[:], in0=wt_sb, scalar1=-1.0, scalar2=0.0, op0=ALU.mult, op1=ALU.add)
+        nc.gpsimd.tensor_scalar(out=neg_wt[:], in0=wt_sb[:], scalar1=-1.0, scalar2=0.0, op0=ALU.mult, op1=ALU.add)
 
         w_codes = [keep.tile([P, HALF], U32, name="w_codes%d" % h, align_bytes=64) for h in range(2)]
         scores = {}
@@ -101,7 +109,10 @@ def tile_attend_gsqh_w_kernel(tc, xT, w_words, w_scales, y, wt, xm, offs, out):
         hinge = [keep.tile([P, PACK, HALF], F32, name="hinge%d" % h, tag="hinge%d" % h, align_bytes=64) for h in range(2)]
         for u in range(2):
             for h in range(2):
-                margin = keep.tile([P, 2, HALF], F32, name="margin", tag="margin%d%d" % (h, u), align_bytes=64)
+                if u + h < 2:
+                    margin = keep.tile([P, 2, HALF], F32, name="margin%d%d" % (h, u), align_bytes=64)
+                else:
+                    margin = shared.tile([P, 2, HALF], F32, name="margin11", align_bytes=64, offset=9216)
                 nc.vector.tensor_tensor(
                     out=margin[:], in0=scores[h, u][:], in1=y_sb[u][:, :, h * HALF : (h + 1) * HALF], op=ALU.mult
                 )
@@ -109,38 +120,20 @@ def tile_attend_gsqh_w_kernel(tc, xT, w_words, w_scales, y, wt, xm, offs, out):
                     out=hinge[h][:, 2 * u : 2 * u + 2, :], in_=margin[:], func=ACT.Relu, bias=1.0, scale=-1.0
                 )
 
-        xm_rows = xm[0].rearrange("(p j) d -> p j d", j=PACK)
-        xm_raw = [
-            keep.tile([P, PACK, D // 2], F32, name="xm_raw%d" % h, tag=tag, align_bytes=64)
-            for h, tag in enumerate(("stage3", "stage2"))
-        ]
-        for h in range(2):
-            nc.sync.dma_start(out=xm_raw[h][:], in_=xm_rows[:, :, h * D // 2 : (h + 1) * D // 2])
-        xm_bf_tags = ("margin11", "hinge1")
-        xm_bf = {}
-        xm_codes = {}
-        xm_codes_tags = ("hinge0", "xm_codes")
-        xm_scale = [keep.tile([P, P], U8, name="xm_scale%d" % k, align_bytes=64) for k in range(D // P)]
+        xm_bf_first = shared.tile([P, P * PACK], BF16, name="xm_bf_first", align_bytes=64, offset=10240)
+        xm_bf_rest = shared.tile([P, 3, P * PACK], BF16, name="xm_bf_rest", align_bytes=64, offset=7168)
+        xm_bf = [xm_bf_first[:]] + [xm_bf_rest[:, k, :] for k in range(3)]
+        xm_scale = keep.tile([P, D], U8, name="xm_scale", align_bytes=64)
+        g_bf = {}
 
         def round_xm(k):
-            if k % 2 == 0:
-                pair = keep.tile([P, 2, P * PACK], BF16, name="xm_bf", tag=xm_bf_tags[k // 2], align_bytes=64)
-                xm_bf[k], xm_bf[k + 1] = pair[:, 0, :], pair[:, 1, :]
             nc.scalar.copy(
                 out=xm_bf[k].rearrange("p (c i j) -> p c j i", i=4, j=PACK),
                 in_=xm_raw[k // 2][:, :, (k % 2) * P : (k % 2 + 1) * P].rearrange("p j (c i) -> p c j i", i=4),
             )
 
-        def quantize_xm(k):
-            if k % 2 == 0:
-                pair = keep.tile([P, 2, P], U32, name="xm_codes", tag=xm_codes_tags[k // 2], align_bytes=64)
-                xm_codes[k], xm_codes[k + 1] = pair[:, 0, :], pair[:, 1, :]
-            nc.vector.quantize_mx(out=xm_codes[k].bitcast(E4M3), scales=xm_scale[k][:], in_=xm_bf[k])
-
-        g_bf = {}
-
-        def make_g(h):
-            g_bf[h] = keep.tile([P, HALF * PACK], BF16, name="g_bf", align_bytes=64)
+        def make_g(h, tile):
+            g_bf[h] = tile
             nc.vector.tensor_tensor(
                 out=g_bf[h][:].rearrange("p (c i t) -> p c t i", i=4, t=PACK),
                 in0=hinge[h][:].rearrange("p t (c i) -> p c t i", i=4),
@@ -156,8 +149,8 @@ def tile_attend_gsqh_w_kernel(tc, xT, w_words, w_scales, y, wt, xm, offs, out):
             acc = psum_dw.tile([P, N], F32, name="acc")
             nc.tensor.matmul_mx(
                 out=acc[:],
-                lhsT=xm_codes[k].bitcast(E4M3),
-                lhsT_scale=xm_scale[k][:],
+                lhsT=xm_codes[:, k * P : (k + 1) * P].bitcast(E4M3),
+                lhsT_scale=xm_scale[:, k * P : (k + 1) * P],
                 rhs=g_codes[:, first : first + N].bitcast(E5M2),
                 rhs_scale=g_scale[:, first : first + N],
                 start=True,
@@ -167,25 +160,27 @@ def tile_attend_gsqh_w_kernel(tc, xT, w_words, w_scales, y, wt, xm, offs, out):
             nc.scalar.copy(out=dw[:], in_=acc[:, keep_from:N])
             return dw
 
-        round_xm(0)
-        round_xm(1)
-        make_g(0)
-        quantize_xm(0)
+        for k in range(D // P):
+            round_xm(k)
+        make_g(0, keep.tile([P, HALF * PACK], BF16, name="g_bf0", align_bytes=64))
+        xm_codes = keep.tile([P, D], U32, name="xm_codes", tag="hinge0", align_bytes=64)
+
+        def quantize_xm(first, last, src):
+            cols = slice(first * P, last * P)
+            nc.vector.quantize_mx(out=xm_codes[:, cols].bitcast(E4M3), scales=xm_scale[:, cols], in_=src)
+
+        quantize_xm(0, 1, xm_bf[0])
         quantize_g(0)
-        make_g(1)
-        quantize_xm(1)
-        early = [gradient(k, 0, HALF, "dw_early%d" % k) for k in range(EARLY)]
+        make_g(1, shared.tile([P, HALF * PACK], BF16, name="g_bf1", align_bytes=64, offset=10240))
+        quantize_xm(1, 2, xm_bf[1])
         quantize_g(1)
-        round_xm(2)
-        round_xm(3)
-        late = [gradient(k, HALF, HALF, "dw_late%d" % k) for k in range(EARLY)]
-        nc.vector.tensor_copy(windows[0][:].indirect(half_offsets[0]), early[0][:])
+        quantize_xm(2, 4, xm_bf_rest[:, 1:3, :].rearrange("p k c -> p (k c)"))
+        early = [gradient(k, 0, HALF, "dw_early%d" % k) for k in range(EARLY)]
+        late = [gradient(k, HALF, HALF if k < EARLY else 0, "dw_late%d" % k) for k in range(D // P)]
+        for k in range(EARLY):
+            nc.vector.tensor_copy(windows[k][:].indirect(half_offsets[0]), early[k][:])
         for k in range(EARLY, D // P):
-            quantize_xm(k)
-            late.append(gradient(k, HALF, 0, "dw_late%d" % k))
-        nc.vector.tensor_copy(windows[1][:].indirect(half_offsets[0]), early[1][:])
-        for k, tag in ((2, "hinge1"), (3, "dw_early1")):
-            window = keep.tile([P, T], F32, name="window%d" % k, tag=tag, align_bytes=64)
+            window = shared.tile([P, T], F32, name="window%d" % k, align_bytes=64, offset=(k - EARLY) * T * 4)
             nc.gpsimd.memset(window[:], 0.0)
             windows.append(window)
         for k in range(D // P):

@@ -19,7 +19,7 @@ N, T, D, R = 512, 2048, 512, 512
 HALF = N // 2
 FLOPS = 2 * 2 * N * D * R
 EARLY = 2
-SPLIT = 48
+SPLIT = 16
 
 
 def tile_attend_gsqh_w_kernel(tc, xT, w_words, w_scales, y, wt, xm, offs, out):
@@ -34,22 +34,22 @@ def tile_attend_gsqh_w_kernel(tc, xT, w_words, w_scales, y, wt, xm, offs, out):
         half_offsets = [offsets[:, h * HALF // 16 : (h + 1) * HALF // 16] for h in range(2)]
 
         table_scales = keep.tile([P, T // 4], I32, name="table_scales", align_bytes=64)
-        nc.vector.memset(table_scales[:], 0)
+        nc.gpsimd.memset(table_scales[:], 0)
         windows = [keep.tile([P, T], F32, name="window%d" % k) for k in range(EARLY)]
         for window in windows:
-            nc.vector.memset(window[:], 0.0)
+            nc.vector.memset(window[:].bitcast(I32), 0)
         g_codes = keep.tile([P, HALF + N], I32, name="g_codes", align_bytes=64)
         g_scale = keep.tile([P, HALF + N], U8, name="g_scale", align_bytes=64)
-        nc.vector.memset(g_codes[:, 0:HALF], 0)
-        nc.vector.memset(g_scale[:, 0:HALF].bitcast(I32), 0)
+        nc.gpsimd.memset(g_codes[:, 0:HALF], 0)
+        nc.gpsimd.memset(g_scale[:, 0:HALF].bitcast(I32), 0)
 
+        nc.sync.dma_start(offsets[:], offs)
         scale_rows = w_scales[0].bitcast(I32)
         staged_scales = keep.tile([P, T // 4], I32, name="staged_scales", align_bytes=64)
         for q in range(4):
             nc.sync.dma_start(out=staged_scales[32 * q : 32 * q + 4, :], in_=scale_rows[4 * q : 4 * q + 4, :])
         xT_raw = keep.tile([P, PACK, R], F32, name="xT_raw", align_bytes=64)
         nc.sync.dma_start(out=xT_raw[:], in_=xT[0].rearrange("(p j) r -> p j r", j=PACK))
-        nc.sync.dma_start(offsets[:], offs)
         table_words = keep.tile([P, T], I32, name="table_words", align_bytes=64)
         nc.sync.dma_start(out=table_words[:], in_=w_words[0].rearrange("p n j -> p (n j)").bitcast(I32))
         wt_sb = keep.tile([P, PACK], F32, name="wt_sb")
@@ -65,15 +65,15 @@ def tile_attend_gsqh_w_kernel(tc, xT, w_words, w_scales, y, wt, xm, offs, out):
 
         for q in range(4):
             nc.vector.tensor_copy(table_scales[32 * q : 32 * q + 4, :], staged_scales[32 * q : 32 * q + 4, :])
+        w_scale = keep.tile([P, N], U8, name="w_scale", align_bytes=64)
+        nc.vector.tensor_copy(w_scale[:], table_scales[:].bitcast(U8).indirect(offsets[:]))
 
-        xT_bf = keep.tile([P, R * PACK], BF16, name="xT_bf", align_bytes=64)
+        xT_bf = keep.tile([P, R * PACK], BF16, name="xT_bf", tag="xT_bf", align_bytes=64)
         xT_bf_by_row = xT_bf[:].rearrange("p (t m j) -> p m j t", t=PACK, j=PACK)
         xT_raw_by_row = xT_raw[:].rearrange("p j (m t) -> p m j t", t=PACK)
         nc.vector.tensor_copy(out=xT_bf_by_row[:, 0:SPLIT], in_=xT_raw_by_row[:, 0:SPLIT])
         nc.scalar.copy(out=xT_bf_by_row[:, SPLIT:P], in_=xT_raw_by_row[:, SPLIT:P])
 
-        w_scale = keep.tile([P, N], U8, name="w_scale", align_bytes=64)
-        nc.vector.tensor_copy(w_scale[:], table_scales[:].bitcast(U8).indirect(offsets[:]))
         xT_codes = keep.tile([P, R], U32, name="xT_codes", align_bytes=64)
         xT_scale = keep.tile([P, R], U8, name="xT_scale", align_bytes=64)
         nc.vector.quantize_mx(out=xT_codes[:].bitcast(E4M3), scales=xT_scale[:], in_=xT_bf[:])
@@ -81,7 +81,10 @@ def tile_attend_gsqh_w_kernel(tc, xT, w_words, w_scales, y, wt, xm, offs, out):
         neg_wt = keep.tile([P, PACK], F32, name="neg_wt")
         nc.gpsimd.tensor_scalar(out=neg_wt[:], in0=wt_sb[:], scalar1=-1.0, scalar2=0.0, op0=ALU.mult, op1=ALU.add)
 
-        w_codes = [keep.tile([P, HALF], U32, name="w_codes%d" % h, align_bytes=64) for h in range(2)]
+        w_codes = [
+            keep.tile([P, HALF], U32, name="w_codes%d" % h, tag=tag, align_bytes=64)
+            for h, tag in enumerate(("w_codes0", "xT_bf"))
+        ]
         scores = {}
         for h in range(2):
             nc.vector.tensor_copy(w_codes[h][:], table_words[:].bitcast(U32).indirect(half_offsets[h]))
@@ -101,7 +104,8 @@ def tile_attend_gsqh_w_kernel(tc, xT, w_words, w_scales, y, wt, xm, offs, out):
                     )
 
         factor = keep.tile([P, PACK, N], F32, name="factor")
-        for t in range(PACK):
+        nc.scalar.activation(out=factor[:, 0, :], in_=y_sb[0][:, 0, :], func=ACT.Copy, scale=neg_wt[:, 0:1])
+        for t in range(1, PACK):
             nc.gpsimd.tensor_scalar(
                 out=factor[:, t, :], in0=y_sb[t // 2][:, t % 2, :], scalar1=neg_wt[:, t : t + 1], scalar2=0.0,
                 op0=ALU.mult, op1=ALU.add,
@@ -179,11 +183,10 @@ def tile_attend_gsqh_w_kernel(tc, xT, w_words, w_scales, y, wt, xm, offs, out):
         late = [gradient(k, HALF, HALF if k < EARLY else 0, "dw_late%d" % k) for k in range(D // P)]
         for k in range(EARLY):
             nc.vector.tensor_copy(windows[k][:].indirect(half_offsets[0]), early[k][:])
-        for k in range(EARLY, D // P):
-            window = shared.tile([P, T], F32, name="window%d" % k, align_bytes=64, offset=(k - EARLY) * T * 4)
-            nc.gpsimd.memset(window[:], 0.0)
-            windows.append(window)
+        window = shared.tile([P, T], F32, name="window2", align_bytes=64, offset=8192)
+        nc.gpsimd.memset(window[:].bitcast(I32), 0)
+        windows.append(window)
         for k in range(D // P):
-            window = windows[k]
+            window = windows[k % 3]
             nc.vector.tensor_copy(window[:].indirect(half_offsets[1] if k < EARLY else offsets[:]), late[k][:])
             nc.sync.dma_start(out=out[k * P : (k + 1) * P, :], in_=window[:])

@@ -19,7 +19,7 @@ N, T, D, R = 512, 2048, 512, 512
 HALF = N // 2
 FLOPS = 2 * 2 * N * D * R
 EARLY = 2
-SPLIT = 16
+SPLIT = 48
 
 
 def tile_attend_gsqh_w_kernel(tc, xT, w_words, w_scales, y, wt, xm, offs, out):
@@ -34,22 +34,21 @@ def tile_attend_gsqh_w_kernel(tc, xT, w_words, w_scales, y, wt, xm, offs, out):
         half_offsets = [offsets[:, h * HALF // 16 : (h + 1) * HALF // 16] for h in range(2)]
 
         table_scales = keep.tile([P, T // 4], I32, name="table_scales", align_bytes=64)
-        nc.gpsimd.memset(table_scales[:], 0)
+        nc.vector.memset(table_scales[:], 0)
         windows = [keep.tile([P, T], F32, name="window%d" % k) for k in range(EARLY)]
         for window in windows:
             nc.vector.memset(window[:].bitcast(I32), 0)
         g_codes = keep.tile([P, HALF + N], I32, name="g_codes", align_bytes=64)
         g_scale = keep.tile([P, HALF + N], U8, name="g_scale", align_bytes=64)
-        nc.gpsimd.memset(g_codes[:, 0:HALF], 0)
-        nc.gpsimd.memset(g_scale[:, 0:HALF].bitcast(I32), 0)
+        nc.vector.memset(g_codes[:, 0:HALF], 0)
+        nc.vector.memset(g_scale[:, 0:HALF].bitcast(I32), 0)
 
         nc.sync.dma_start(offsets[:], offs)
-        scale_rows = w_scales[0].bitcast(I32)
-        staged_scales = keep.tile([P, T // 4], I32, name="staged_scales", align_bytes=64)
-        for q in range(4):
-            nc.sync.dma_start(out=staged_scales[32 * q : 32 * q + 4, :], in_=scale_rows[4 * q : 4 * q + 4, :])
         xT_raw = keep.tile([P, PACK, R], F32, name="xT_raw", align_bytes=64)
         nc.sync.dma_start(out=xT_raw[:], in_=xT[0].rearrange("(p j) r -> p j r", j=PACK))
+        scale_rows = w_scales[0].bitcast(I32)
+        for q in range(4):
+            nc.sync.dma_start(out=table_scales[32 * q : 32 * q + 4, :], in_=scale_rows[4 * q : 4 * q + 4, :])
         table_words = keep.tile([P, T], I32, name="table_words", align_bytes=64)
         nc.sync.dma_start(out=table_words[:], in_=w_words[0].rearrange("p n j -> p (n j)").bitcast(I32))
         wt_sb = keep.tile([P, PACK], F32, name="wt_sb")
@@ -63,17 +62,15 @@ def tile_attend_gsqh_w_kernel(tc, xT, w_words, w_scales, y, wt, xm, offs, out):
         for h in range(2):
             nc.sync.dma_start(out=xm_raw[h][:], in_=xm_rows[:, :, h * D // 2 : (h + 1) * D // 2])
 
-        for q in range(4):
-            nc.vector.tensor_copy(table_scales[32 * q : 32 * q + 4, :], staged_scales[32 * q : 32 * q + 4, :])
-        w_scale = keep.tile([P, N], U8, name="w_scale", align_bytes=64)
-        nc.vector.tensor_copy(w_scale[:], table_scales[:].bitcast(U8).indirect(offsets[:]))
 
-        xT_bf = keep.tile([P, R * PACK], BF16, name="xT_bf", tag="xT_bf", align_bytes=64)
+        xT_bf = shared.tile([P, R * PACK], BF16, name="xT_bf", align_bytes=64, offset=16384)
         xT_bf_by_row = xT_bf[:].rearrange("p (t m j) -> p m j t", t=PACK, j=PACK)
         xT_raw_by_row = xT_raw[:].rearrange("p j (m t) -> p m j t", t=PACK)
         nc.vector.tensor_copy(out=xT_bf_by_row[:, 0:SPLIT], in_=xT_raw_by_row[:, 0:SPLIT])
         nc.scalar.copy(out=xT_bf_by_row[:, SPLIT:P], in_=xT_raw_by_row[:, SPLIT:P])
 
+        w_scale = keep.tile([P, N], U8, name="w_scale", align_bytes=64)
+        nc.vector.tensor_copy(w_scale[:], table_scales[:].bitcast(U8).indirect(offsets[:]))
         xT_codes = keep.tile([P, R], U32, name="xT_codes", align_bytes=64)
         xT_scale = keep.tile([P, R], U8, name="xT_scale", align_bytes=64)
         nc.vector.quantize_mx(out=xT_codes[:].bitcast(E4M3), scales=xT_scale[:], in_=xT_bf[:])
@@ -82,8 +79,8 @@ def tile_attend_gsqh_w_kernel(tc, xT, w_words, w_scales, y, wt, xm, offs, out):
         nc.gpsimd.tensor_scalar(out=neg_wt[:], in0=wt_sb[:], scalar1=-1.0, scalar2=0.0, op0=ALU.mult, op1=ALU.add)
 
         w_codes = [
-            keep.tile([P, HALF], U32, name="w_codes%d" % h, tag=tag, align_bytes=64)
-            for h, tag in enumerate(("w_codes0", "xT_bf"))
+            shared.tile([P, HALF], U32, name="w_codes%d" % h, align_bytes=64, offset=16384 + h * HALF * 4)
+            for h in range(2)
         ]
         scores = {}
         for h in range(2):
@@ -104,8 +101,7 @@ def tile_attend_gsqh_w_kernel(tc, xT, w_words, w_scales, y, wt, xm, offs, out):
                     )
 
         factor = keep.tile([P, PACK, N], F32, name="factor")
-        nc.scalar.activation(out=factor[:, 0, :], in_=y_sb[0][:, 0, :], func=ACT.Copy, scale=neg_wt[:, 0:1])
-        for t in range(1, PACK):
+        for t in range(PACK):
             nc.gpsimd.tensor_scalar(
                 out=factor[:, t, :], in0=y_sb[t // 2][:, t % 2, :], scalar1=neg_wt[:, t : t + 1], scalar2=0.0,
                 op0=ALU.mult, op1=ALU.add,

@@ -75,50 +75,65 @@ def tile_attend_gsqh_w_kernel(tc, xT, w_words, w_scales, y, wt, xm, offs, out):
         xT_scale = keep.tile([P, R], U8, name="xT_scale", align_bytes=64)
         nc.vector.quantize_mx(out=xT_codes[:].bitcast(E4M3), scales=xT_scale[:], in_=xT_bf[:])
 
-        neg_wt = keep.tile([P, PACK], F32, name="neg_wt")
-        nc.gpsimd.tensor_scalar(out=neg_wt[:], in0=wt_sb[:], scalar1=-1.0, scalar2=0.0, op0=ALU.mult, op1=ALU.add)
+        neg_wt = shared.tile([P, 2], F32, name="neg_wt", offset=8192)
+        nc.scalar.activation(out=neg_wt[:], in_=wt_sb[:, 0:PACK:2], func=ACT.Copy, scale=-1.0)
 
         w_codes = [
             shared.tile([P, HALF], U32, name="w_codes%d" % h, align_bytes=64, offset=16384 + h * HALF * 4)
             for h in range(2)
         ]
-        scores = {}
         for h in range(2):
             nc.vector.tensor_copy(w_codes[h][:], table_words[:].bitcast(U32).indirect(half_offsets[h]))
-        for u in range(2):
-            for h in range(2):
-                scores[h, u] = psum.tile([P, 2, HALF], F32, name="scores%d%d" % (h, u))
-                for e in range(2):
-                    t = 2 * u + e
-                    nc.tensor.matmul_mx(
-                        out=scores[h, u][:, e, :],
-                        lhsT=xT_codes[:, t * P : (t + 1) * P].bitcast(E4M3),
-                        lhsT_scale=xT_scale[:, t * P : (t + 1) * P],
-                        rhs=w_codes[h][:].bitcast(E4M3),
-                        rhs_scale=w_scale[:, h * HALF : (h + 1) * HALF],
-                        start=True,
-                        stop=True,
-                    )
+        banks = [(0, 0, 2), (0, 2, 4), (1, 2, 4), (1, 0, 2)]
+        scores = {}
+        for h, t0, t1 in banks:
+            bank = psum.tile([P, 2, HALF], F32, name="scores%d%d" % (h, t0))
+            for t in range(t0, t1):
+                scores[h, t] = (bank, t - t0)
+                nc.tensor.matmul_mx(
+                    out=bank[:, t - t0, :],
+                    lhsT=xT_codes[:, t * P : (t + 1) * P].bitcast(E4M3),
+                    lhsT_scale=xT_scale[:, t * P : (t + 1) * P],
+                    rhs=w_codes[h][:].bitcast(E4M3),
+                    rhs_scale=w_scale[:, h * HALF : (h + 1) * HALF],
+                    start=True,
+                    stop=True,
+                )
 
         factor = keep.tile([P, PACK, N], F32, name="factor")
-        for t in range(PACK):
+        nc.scalar.activation(out=factor[:, 0, :], in_=y_sb[0][:, 0, :], func=ACT.Copy, scale=neg_wt[:, 0:1])
+        for t in range(1, PACK):
+            weight, sign = (neg_wt[:, 1:2], 1.0) if t == 2 else (wt_sb[:, t : t + 1], -1.0)
             nc.gpsimd.tensor_scalar(
-                out=factor[:, t, :], in0=y_sb[t // 2][:, t % 2, :], scalar1=neg_wt[:, t : t + 1], scalar2=0.0,
-                op0=ALU.mult, op1=ALU.add,
+                out=factor[:, t, :], in0=y_sb[t // 2][:, t % 2, :], scalar1=weight, scalar2=sign,
+                op0=ALU.mult, op1=ALU.mult,
             )
         hinge = [keep.tile([P, PACK, HALF], F32, name="hinge%d" % h, tag="hinge%d" % h, align_bytes=64) for h in range(2)]
-        for u in range(2):
-            for h in range(2):
-                if u + h < 2:
-                    margin = keep.tile([P, 2, HALF], F32, name="margin%d%d" % (h, u), align_bytes=64)
-                else:
-                    margin = shared.tile([P, 2, HALF], F32, name="margin11", align_bytes=64, offset=9216)
-                nc.vector.tensor_tensor(
-                    out=margin[:], in0=scores[h, u][:], in1=y_sb[u][:, :, h * HALF : (h + 1) * HALF], op=ALU.mult
-                )
-                nc.scalar.activation(
-                    out=hinge[h][:, 2 * u : 2 * u + 2, :], in_=margin[:], func=ACT.Relu, bias=1.0, scale=-1.0
-                )
+        steps = banks
+        margins = {}
+        for h, t0, t1 in steps:
+            if (h, t1) == (1, 2):
+                margins[h, t0] = shared.tile([P, t1 - t0, HALF], F32, name="margin_last", align_bytes=64, offset=8192)
+            elif (h, t1) == (0, 4):
+                margins[h, t0] = shared.tile([P, t1 - t0, HALF], F32, name="margin_mid", align_bytes=64, offset=10240)
+            else:
+                margins[h, t0] = keep.tile([P, t1 - t0, HALF], F32, name="margin%d%d" % (h, t0), align_bytes=64)
+
+        def make_margin(h, t0, t1):
+            bank, e = scores[h, t0]
+            nc.vector.tensor_tensor(
+                out=margins[h, t0][:], in0=bank[:, e : e + t1 - t0, :],
+                in1=y_sb[t0 // 2][:, t0 % 2 : t0 % 2 + t1 - t0, h * HALF : (h + 1) * HALF], op=ALU.mult,
+            )
+
+        def make_hinge(h, t0, t1):
+            nc.scalar.activation(out=hinge[h][:, t0:t1, :], in_=margins[h, t0][:], func=ACT.Relu, bias=1.0, scale=-1.0)
+
+        for step in steps[:2]:
+            make_margin(*step)
+            make_hinge(*step)
+        for step in steps[2:]:
+            make_margin(*step)
 
         xm_bf_first = shared.tile([P, P * PACK], BF16, name="xm_bf_first", align_bytes=64, offset=10240)
         xm_bf_rest = shared.tile([P, 3, P * PACK], BF16, name="xm_bf_rest", align_bytes=64, offset=7168)
@@ -160,7 +175,10 @@ def tile_attend_gsqh_w_kernel(tc, xT, w_words, w_scales, y, wt, xm, offs, out):
             nc.scalar.copy(out=dw[:], in_=acc[:, keep_from:N])
             return dw
 
-        for k in range(D // P):
+        round_xm(0)
+        for step in steps[2:]:
+            make_hinge(*step)
+        for k in range(1, D // P):
             round_xm(k)
         make_g(0, keep.tile([P, HALF * PACK], BF16, name="g_bf0", align_bytes=64))
         xm_codes = keep.tile([P, D], U32, name="xm_codes", tag="hinge0", align_bytes=64)

@@ -43,9 +43,9 @@ def tile_attend_gsqh_w_kernel(tc, xT, w_words, w_scales, y, wt, xm, offs, out):
         nc.vector.memset(g_codes[:, 0:HALF], 0)
         nc.vector.memset(g_scale[:, 0:HALF].bitcast(I32), 0)
 
-        nc.sync.dma_start(offsets[:], offs)
         xT_raw = keep.tile([P, PACK, R], F32, name="xT_raw", align_bytes=64)
         nc.sync.dma_start(out=xT_raw[:], in_=xT[0].rearrange("(p j) r -> p j r", j=PACK))
+        nc.sync.dma_start(offsets[:], offs)
         scale_rows = w_scales[0].bitcast(I32)
         for q in range(4):
             nc.sync.dma_start(out=table_scales[32 * q : 32 * q + 4, :], in_=scale_rows[4 * q : 4 * q + 4, :])
@@ -178,8 +178,11 @@ def tile_attend_gsqh_w_kernel(tc, xT, w_words, w_scales, y, wt, xm, offs, out):
         round_xm(0)
         for step in steps[2:]:
             make_hinge(*step)
-        for k in range(1, D // P):
-            round_xm(k)
+        round_xm(1)
+        nc.scalar.copy(
+            out=xm_bf_rest[:, 1:3, :].rearrange("p k (c i j) -> p (k c) j i", i=4, j=PACK),
+            in_=xm_raw[1][:].rearrange("p j (c i) -> p c j i", i=4),
+        )
         make_g(0, keep.tile([P, HALF * PACK], BF16, name="g_bf0", align_bytes=64))
         xm_codes = keep.tile([P, D], U32, name="xm_codes", tag="hinge0", align_bytes=64)
 

@@ -58,9 +58,11 @@ def tile_attend_gsqh_w_kernel(tc, xT, w_words, w_scales, y, wt, xm, offs, out):
         for u in range(2):
             nc.sync.dma_start(out=y_sb[u][:], in_=y_rows[:, 2 * u : 2 * u + 2, :])
         xm_rows = xm[0].rearrange("(p j) d -> p j d", j=PACK)
-        xm_raw = [keep.tile([P, PACK, D // 2], F32, name="xm_raw%d" % h, align_bytes=64) for h in range(2)]
-        for h in range(2):
-            nc.sync.dma_start(out=xm_raw[h][:], in_=xm_rows[:, :, h * D // 2 : (h + 1) * D // 2])
+        xm_first = keep.tile([P, PACK, P], F32, name="xm_first", align_bytes=64)
+        xm_rest = keep.tile([P, PACK, D - P], F32, name="xm_rest", align_bytes=64)
+        nc.sync.dma_start(out=xm_first[:], in_=xm_rows[:, :, 0:P])
+        nc.sync.dma_start(out=xm_rest[:], in_=xm_rows[:, :, P:D])
+        xm_raw = [xm_first[:], xm_rest[:, :, 0:P]]
 
 
         xT_bf = shared.tile([P, R * PACK], BF16, name="xT_bf", align_bytes=64, offset=16384)
@@ -144,7 +146,7 @@ def tile_attend_gsqh_w_kernel(tc, xT, w_words, w_scales, y, wt, xm, offs, out):
         def round_xm(k):
             nc.scalar.copy(
                 out=xm_bf[k].rearrange("p (c i j) -> p c j i", i=4, j=PACK),
-                in_=xm_raw[k // 2][:, :, (k % 2) * P : (k % 2 + 1) * P].rearrange("p j (c i) -> p c j i", i=4),
+                in_=xm_raw[k].rearrange("p j (c i) -> p c j i", i=4),
             )
 
         def make_g(h, tile):
@@ -181,7 +183,7 @@ def tile_attend_gsqh_w_kernel(tc, xT, w_words, w_scales, y, wt, xm, offs, out):
         round_xm(1)
         nc.scalar.copy(
             out=xm_bf_rest[:, 1:3, :].rearrange("p k (c i j) -> p (k c) j i", i=4, j=PACK),
-            in_=xm_raw[1][:].rearrange("p j (c i) -> p c j i", i=4),
+            in_=xm_rest[:, :, P : D - P].rearrange("p j (c i) -> p c j i", i=4),
         )
         make_g(0, keep.tile([P, HALF * PACK], BF16, name="g_bf0", align_bytes=64))
         xm_codes = keep.tile([P, D], U32, name="xm_codes", tag="hinge0", align_bytes=64)

@@ -62,7 +62,7 @@ def tile_attend_gsqh_w_kernel(tc, xT, w_words, w_scales, y, wt, xm, offs, out):
         xm_rest = keep.tile([P, PACK, D - P], F32, name="xm_rest", align_bytes=64)
         nc.sync.dma_start(out=xm_first[:], in_=xm_rows[:, :, 0:P])
         nc.sync.dma_start(out=xm_rest[:], in_=xm_rows[:, :, P:D])
-        xm_raw = [xm_first[:], xm_rest[:, :, 0:P]]
+        xm_raw = [xm_first[:]] + [xm_rest[:, :, k * P : (k + 1) * P] for k in range(3)]
 
 
         xT_bf = shared.tile([P, R * PACK], BF16, name="xT_bf", align_bytes=64, offset=16384)
@@ -138,8 +138,8 @@ def tile_attend_gsqh_w_kernel(tc, xT, w_words, w_scales, y, wt, xm, offs, out):
             make_margin(*step)
 
         xm_bf_first = shared.tile([P, P * PACK], BF16, name="xm_bf_first", align_bytes=64, offset=10240)
-        xm_bf_rest = shared.tile([P, 3, P * PACK], BF16, name="xm_bf_rest", align_bytes=64, offset=7168)
-        xm_bf = [xm_bf_first[:]] + [xm_bf_rest[:, k, :] for k in range(3)]
+        xm_bf_mid = shared.tile([P, 2, P * PACK], BF16, name="xm_bf_mid", align_bytes=64, offset=6400)
+        xm_bf = [xm_bf_first[:]] + [xm_bf_mid[:, k, :] for k in range(2)]
         xm_scale = keep.tile([P, D], U8, name="xm_scale", align_bytes=64)
         g_bf = {}
 
@@ -180,10 +180,9 @@ def tile_attend_gsqh_w_kernel(tc, xT, w_words, w_scales, y, wt, xm, offs, out):
         round_xm(0)
         for step in steps[2:]:
             make_hinge(*step)
-        round_xm(1)
         nc.scalar.copy(
-            out=xm_bf_rest[:, 1:3, :].rearrange("p k (c i j) -> p (k c) j i", i=4, j=PACK),
-            in_=xm_rest[:, :, P : D - P].rearrange("p j (c i) -> p c j i", i=4),
+            out=xm_bf_mid[:].rearrange("p k (c i j) -> p (k c) j i", i=4, j=PACK),
+            in_=xm_rest[:, :, 0 : 2 * P].rearrange("p j (c i) -> p c j i", i=4),
         )
         make_g(0, keep.tile([P, HALF * PACK], BF16, name="g_bf0", align_bytes=64))
         xm_codes = keep.tile([P, D], U32, name="xm_codes", tag="hinge0", align_bytes=64)
@@ -195,10 +194,13 @@ def tile_attend_gsqh_w_kernel(tc, xT, w_words, w_scales, y, wt, xm, offs, out):
         quantize_xm(0, 1, xm_bf[0])
         quantize_g(0)
         make_g(1, shared.tile([P, HALF * PACK], BF16, name="g_bf1", align_bytes=64, offset=10240))
-        quantize_xm(1, 2, xm_bf[1])
+        quantize_xm(1, 3, xm_bf_mid[:].rearrange("p k c -> p (k c)"))
         quantize_g(1)
-        quantize_xm(2, 4, xm_bf_rest[:, 1:3, :].rearrange("p k c -> p (k c)"))
         early = [gradient(k, 0, HALF, "dw_early%d" % k) for k in range(EARLY)]
+        xm_bf_last = shared.tile([P, P * PACK], BF16, name="xm_bf_last", align_bytes=64, offset=10240)
+        xm_bf.append(xm_bf_last[:])
+        round_xm(3)
+        quantize_xm(3, 4, xm_bf[3])
         late = [gradient(k, HALF, HALF if k < EARLY else 0, "dw_late%d" % k) for k in range(D // P)]
         for k in range(EARLY):
             nc.vector.tensor_copy(windows[k][:].indirect(half_offsets[0]), early[k][:])

@@ -55,8 +55,9 @@ def tile_attend_gsqh_w_kernel(tc, xT, w_words, w_scales, y, wt, xm, offs, out):
         nc.sync.dma_start(out=wt_sb[:], in_=wt[0].rearrange("(p t) o -> p (t o)", t=PACK))
         y_rows = y[0].rearrange("(p t) n -> p t n", t=PACK)
         y_sb = [keep.tile([P, 2, N], F32, name="y_sb%d" % u, align_bytes=64) for u in range(2)]
-        for u in range(2):
-            nc.sync.dma_start(out=y_sb[u][:], in_=y_rows[:, 2 * u : 2 * u + 2, :])
+        nc.sync.dma_start(out=y_sb[0][:], in_=y_rows[:, 0:2, :])
+        for t in range(2, PACK):
+            nc.sync.dma_start(out=y_sb[1][:, t - 2, :], in_=y_rows[:, t, :])
         xm_rows = xm[0].rearrange("(p j) d -> p j d", j=PACK)
         xm_first = keep.tile([P, PACK, P], F32, name="xm_first", align_bytes=64)
         xm_rest = keep.tile([P, PACK, D - P], F32, name="xm_rest", align_bytes=64)
@@ -123,10 +124,12 @@ def tile_attend_gsqh_w_kernel(tc, xT, w_words, w_scales, y, wt, xm, offs, out):
 
         def make_margin(h, t0, t1):
             bank, e = scores[h, t0]
-            nc.vector.tensor_tensor(
-                out=margins[h, t0][:], in0=bank[:, e : e + t1 - t0, :],
-                in1=y_sb[t0 // 2][:, t0 % 2 : t0 % 2 + t1 - t0, h * HALF : (h + 1) * HALF], op=ALU.mult,
-            )
+            width = 1 if (h, t0) == (0, 2) else t1 - t0
+            for c in range(0, t1 - t0, width):
+                nc.vector.tensor_tensor(
+                    out=margins[h, t0][:, c : c + width, :], in0=bank[:, e + c : e + c + width, :],
+                    in1=y_sb[t0 // 2][:, t0 % 2 + c : t0 % 2 + c + width, h * HALF : (h + 1) * HALF], op=ALU.mult,
+                )
 
         def make_hinge(h, t0, t1):
             nc.scalar.activation(out=hinge[h][:, t0:t1, :], in_=margins[h, t0][:], func=ACT.Relu, bias=1.0, scale=-1.0)
@@ -210,4 +213,7 @@ def tile_attend_gsqh_w_kernel(tc, xT, w_words, w_scales, y, wt, xm, offs, out):
         for k in range(D // P):
             window = windows[k % 3]
             nc.vector.tensor_copy(window[:].indirect(half_offsets[1] if k < EARLY else offsets[:]), late[k][:])
-            nc.sync.dma_start(out=out[k * P : (k + 1) * P, :], in_=window[:])
+            pieces = (4, 4, 2, 1)[k]
+            for u in range(pieces):
+                cols = slice(u * T // pieces, (u + 1) * T // pieces)
+                nc.sync.dma_start(out=out[k * P : (k + 1) * P, cols], in_=window[:, cols])

@@ -54,16 +54,23 @@ def tile_attend_gsqh_w_kernel(tc, xT, w_words, w_scales, y, wt, xm, offs, out):
         wt_sb = keep.tile([P, PACK], F32, name="wt_sb")
         nc.sync.dma_start(out=wt_sb[:], in_=wt[0].rearrange("(p t) o -> p (t o)", t=PACK))
         y_rows = y[0].rearrange("(p t) n -> p t n", t=PACK)
-        y_sb = [keep.tile([P, 2, N], F32, name="y_sb%d" % u, align_bytes=64) for u in range(2)]
-        nc.sync.dma_start(out=y_sb[0][:], in_=y_rows[:, 0:2, :])
-        for t in range(2, PACK):
-            nc.sync.dma_start(out=y_sb[1][:, t - 2, :], in_=y_rows[:, t, :])
+        y_low = keep.tile([P, 2, N], F32, name="y_low", align_bytes=64)
+        for t in range(2):
+            nc.sync.dma_start(out=y_low[:, t, :], in_=y_rows[:, t, :])
+        y_high = [
+            shared.tile([P, 2, HALF], F32, name="y_high0", align_bytes=64, offset=8192),
+            keep.tile([P, 2, HALF], F32, name="y_high1", align_bytes=64),
+        ]
+        for h in range(2):
+            nc.sync.dma_start(out=y_high[h][:], in_=y_rows[:, 2:PACK, h * HALF : (h + 1) * HALF])
         xm_rows = xm[0].rearrange("(p j) d -> p j d", j=PACK)
         xm_first = keep.tile([P, PACK, P], F32, name="xm_first", align_bytes=64)
-        xm_rest = keep.tile([P, PACK, D - P], F32, name="xm_rest", align_bytes=64)
+        xm_rest = keep.tile([P, PACK, 2 * P], F32, name="xm_rest", align_bytes=64)
+        xm_last = keep.tile([P, PACK, P], F32, name="xm_last", align_bytes=64)
         nc.sync.dma_start(out=xm_first[:], in_=xm_rows[:, :, 0:P])
-        nc.sync.dma_start(out=xm_rest[:], in_=xm_rows[:, :, P:D])
-        xm_raw = [xm_first[:]] + [xm_rest[:, :, k * P : (k + 1) * P] for k in range(3)]
+        nc.sync.dma_start(out=xm_rest[:], in_=xm_rows[:, :, P : D - P])
+        nc.sync.dma_start(out=xm_last[:], in_=xm_rows[:, :, D - P : D])
+        xm_raw = {0: xm_first[:], 3: xm_last[:]}
 
 
         xT_bf = shared.tile([P, R * PACK], BF16, name="xT_bf", align_bytes=64, offset=16384)
@@ -78,8 +85,8 @@ def tile_attend_gsqh_w_kernel(tc, xT, w_words, w_scales, y, wt, xm, offs, out):
         xT_scale = keep.tile([P, R], U8, name="xT_scale", align_bytes=64)
         nc.vector.quantize_mx(out=xT_codes[:].bitcast(E4M3), scales=xT_scale[:], in_=xT_bf[:])
 
-        neg_wt = shared.tile([P, 2], F32, name="neg_wt", offset=8192)
-        nc.scalar.activation(out=neg_wt[:], in_=wt_sb[:, 0:PACK:2], func=ACT.Copy, scale=-1.0)
+        neg_wt = keep.tile([P, 2], F32, name="neg_wt")
+        nc.scalar.activation(out=neg_wt[:], in_=wt_sb[:, 1:PACK:2], func=ACT.Copy, scale=-1.0)
 
         w_codes = [
             shared.tile([P, HALF], U32, name="w_codes%d" % h, align_bytes=64, offset=16384 + h * HALF * 4)
@@ -104,12 +111,17 @@ def tile_attend_gsqh_w_kernel(tc, xT, w_words, w_scales, y, wt, xm, offs, out):
                 )
 
         factor = keep.tile([P, PACK, N], F32, name="factor")
-        nc.scalar.activation(out=factor[:, 0, :], in_=y_sb[0][:, 0, :], func=ACT.Copy, scale=neg_wt[:, 0:1])
-        for t in range(1, PACK):
-            weight, sign = (neg_wt[:, 1:2], 1.0) if t == 2 else (wt_sb[:, t : t + 1], -1.0)
+        first, second = slice(0, HALF), slice(HALF, N)
+        nc.scalar.activation(out=factor[:, 1, :], in_=y_low[:, 1, :], func=ACT.Copy, scale=neg_wt[:, 0:1])
+        nc.scalar.activation(out=factor[:, 3, first], in_=y_high[0][:, 1, :], func=ACT.Copy, scale=neg_wt[:, 1:2])
+        for t, cols, src in (
+            (0, slice(0, N), y_low[:, 0, :]),
+            (2, first, y_high[0][:, 0, :]),
+            (2, second, y_high[1][:, 0, :]),
+            (3, second, y_high[1][:, 1, :]),
+        ):
             nc.gpsimd.tensor_scalar(
-                out=factor[:, t, :], in0=y_sb[t // 2][:, t % 2, :], scalar1=weight, scalar2=sign,
-                op0=ALU.mult, op1=ALU.mult,
+                out=factor[:, t, cols], in0=src, scalar1=wt_sb[:, t : t + 1], scalar2=-1.0, op0=ALU.mult, op1=ALU.mult
             )
         hinge = [keep.tile([P, PACK, HALF], F32, name="hinge%d" % h, tag="hinge%d" % h, align_bytes=64) for h in range(2)]
         steps = banks
@@ -124,12 +136,10 @@ def tile_attend_gsqh_w_kernel(tc, xT, w_words, w_scales, y, wt, xm, offs, out):
 
         def make_margin(h, t0, t1):
             bank, e = scores[h, t0]
-            width = 1 if (h, t0) == (0, 2) else t1 - t0
-            for c in range(0, t1 - t0, width):
-                nc.vector.tensor_tensor(
-                    out=margins[h, t0][:, c : c + width, :], in0=bank[:, e + c : e + c + width, :],
-                    in1=y_sb[t0 // 2][:, t0 % 2 + c : t0 % 2 + c + width, h * HALF : (h + 1) * HALF], op=ALU.mult,
-                )
+            nc.vector.tensor_tensor(
+                out=margins[h, t0][:], in0=bank[:, e : e + t1 - t0, :],
+                in1=y_low[:, :, h * HALF : (h + 1) * HALF] if t0 == 0 else y_high[h][:], op=ALU.mult,
+            )
 
         def make_hinge(h, t0, t1):
             nc.scalar.activation(out=hinge[h][:, t0:t1, :], in_=margins[h, t0][:], func=ACT.Relu, bias=1.0, scale=-1.0)
@@ -185,7 +195,7 @@ def tile_attend_gsqh_w_kernel(tc, xT, w_words, w_scales, y, wt, xm, offs, out):
             make_hinge(*step)
         nc.scalar.copy(
             out=xm_bf_mid[:].rearrange("p k (c i j) -> p (k c) j i", i=4, j=PACK),
-            in_=xm_rest[:, :, 0 : 2 * P].rearrange("p j (c i) -> p c j i", i=4),
+            in_=xm_rest[:].rearrange("p j (c i) -> p c j i", i=4),
         )
         make_g(0, keep.tile([P, HALF * PACK], BF16, name="g_bf0", align_bytes=64))
         xm_codes = keep.tile([P, D], U32, name="xm_codes", tag="hinge0", align_bytes=64)
@@ -213,7 +223,7 @@ def tile_attend_gsqh_w_kernel(tc, xT, w_words, w_scales, y, wt, xm, offs, out):
         for k in range(D // P):
             window = windows[k % 3]
             nc.vector.tensor_copy(window[:].indirect(half_offsets[1] if k < EARLY else offsets[:]), late[k][:])
-            pieces = (4, 4, 2, 1)[k]
+            pieces = (4, 2, 2, 1)[k]
             for u in range(pieces):
                 cols = slice(u * T // pieces, (u + 1) * T // pieces)
                 nc.sync.dma_start(out=out[k * P : (k + 1) * P, cols], in_=window[:, cols])

@@ -17,8 +17,8 @@ P = 128
 PACK = 4
 N, T, D, R = 512, 2048, 512, 512
 HALF = N // 2
+QUARTER = N // 4
 FLOPS = 2 * 2 * N * D * R
-EARLY = 2
 SPLIT = 48
 
 
@@ -31,17 +31,17 @@ def tile_attend_gsqh_w_kernel(tc, xT, w_words, w_scales, y, wt, xm, offs, out):
         psum_dw = ctx.enter_context(tc.psum_pool(name="psum_dw", bufs=4))
 
         offsets = keep.tile([P, N // 16], U16, name="offsets")
-        half_offsets = [offsets[:, h * HALF // 16 : (h + 1) * HALF // 16] for h in range(2)]
+        halves = [slice(h * HALF, (h + 1) * HALF) for h in range(2)]
+        quarters = [slice(q * QUARTER, (q + 1) * QUARTER) for q in range(4)]
+
+        def listed(slots):
+            return offsets[:, slots.start // 16 : slots.stop // 16]
 
         table_scales = keep.tile([P, T // 4], I32, name="table_scales", align_bytes=64)
         nc.vector.memset(table_scales[:], 0)
-        windows = [keep.tile([P, T], F32, name="window%d" % k) for k in range(EARLY)]
+        windows = [keep.tile([P, T], F32, name="window%d" % k) for k in range(2)]
         for window in windows:
             nc.vector.memset(window[:].bitcast(I32), 0)
-        g_codes = keep.tile([P, HALF + N], I32, name="g_codes", align_bytes=64)
-        g_scale = keep.tile([P, HALF + N], U8, name="g_scale", align_bytes=64)
-        nc.vector.memset(g_codes[:, 0:HALF], 0)
-        nc.vector.memset(g_scale[:, 0:HALF].bitcast(I32), 0)
 
         xT_raw = keep.tile([P, PACK, R], F32, name="xT_raw", align_bytes=64)
         nc.sync.dma_start(out=xT_raw[:], in_=xT[0].rearrange("(p j) r -> p j r", j=PACK))
@@ -54,24 +54,15 @@ def tile_attend_gsqh_w_kernel(tc, xT, w_words, w_scales, y, wt, xm, offs, out):
         wt_sb = keep.tile([P, PACK], F32, name="wt_sb")
         nc.sync.dma_start(out=wt_sb[:], in_=wt[0].rearrange("(p t) o -> p (t o)", t=PACK))
         y_rows = y[0].rearrange("(p t) n -> p t n", t=PACK)
-        y_low = keep.tile([P, 2, N], F32, name="y_low", align_bytes=64)
-        for t in range(2):
-            nc.sync.dma_start(out=y_low[:, t, :], in_=y_rows[:, t, :])
-        y_high = [
-            shared.tile([P, 2, HALF], F32, name="y_high0", align_bytes=64, offset=8192),
-            keep.tile([P, 2, HALF], F32, name="y_high1", align_bytes=64),
-        ]
+        labels = [keep.tile([P, PACK, HALF], F32, name="labels%d" % h, align_bytes=64) for h in range(2)]
         for h in range(2):
-            nc.sync.dma_start(out=y_high[h][:], in_=y_rows[:, 2:PACK, h * HALF : (h + 1) * HALF])
+            nc.sync.dma_start(out=labels[h][:], in_=y_rows[:, :, halves[h]])
         xm_rows = xm[0].rearrange("(p j) d -> p j d", j=PACK)
-        xm_first = keep.tile([P, PACK, P], F32, name="xm_first", align_bytes=64)
-        xm_rest = keep.tile([P, PACK, 2 * P], F32, name="xm_rest", align_bytes=64)
-        xm_last = keep.tile([P, PACK, P], F32, name="xm_last", align_bytes=64)
+        xm_first = shared.tile([P, PACK, P], F32, name="xm_first", align_bytes=64, offset=0)
         nc.sync.dma_start(out=xm_first[:], in_=xm_rows[:, :, 0:P])
-        nc.sync.dma_start(out=xm_rest[:], in_=xm_rows[:, :, P : D - P])
-        nc.sync.dma_start(out=xm_last[:], in_=xm_rows[:, :, D - P : D])
-        xm_raw = {0: xm_first[:], 3: xm_last[:]}
-
+        xm_rest = shared.tile([P, PACK, D - P], F32, name="xm_rest", align_bytes=64, offset=24576)
+        nc.sync.dma_start(out=xm_rest[:], in_=xm_rows[:, :, P:D])
+        xm_raw = [xm_first[:]] + [xm_rest[:, :, k * P : (k + 1) * P] for k in range(3)]
 
         xT_bf = shared.tile([P, R * PACK], BF16, name="xT_bf", align_bytes=64, offset=16384)
         xT_bf_by_row = xT_bf[:].rearrange("p (t m j) -> p m j t", t=PACK, j=PACK)
@@ -88,142 +79,169 @@ def tile_attend_gsqh_w_kernel(tc, xT, w_words, w_scales, y, wt, xm, offs, out):
         neg_wt = keep.tile([P, 2], F32, name="neg_wt")
         nc.scalar.activation(out=neg_wt[:], in_=wt_sb[:, 1:PACK:2], func=ACT.Copy, scale=-1.0)
 
-        w_codes = [
-            shared.tile([P, HALF], U32, name="w_codes%d" % h, align_bytes=64, offset=16384 + h * HALF * 4)
-            for h in range(2)
-        ]
-        for h in range(2):
-            nc.vector.tensor_copy(w_codes[h][:], table_words[:].bitcast(U32).indirect(half_offsets[h]))
-        banks = [(0, 0, 2), (0, 2, 4), (1, 2, 4), (1, 0, 2)]
-        scores = {}
-        for h, t0, t1 in banks:
-            bank = psum.tile([P, 2, HALF], F32, name="scores%d%d" % (h, t0))
-            for t in range(t0, t1):
-                scores[h, t] = (bank, t - t0)
+        w_first = shared.tile([P, QUARTER], U32, name="w_first", align_bytes=64, offset=16384)
+        w_second = shared.tile([P, QUARTER], U32, name="w_second", align_bytes=64, offset=16384 + 512)
+        w_rest = shared.tile([P, HALF], U32, name="w_rest", align_bytes=64, offset=16384 + 1024)
+        for codes, slots in ((w_first, quarters[0]), (w_second, quarters[1]), (w_rest, halves[1])):
+            nc.vector.tensor_copy(codes[:], table_words[:].bitcast(U32).indirect(listed(slots)))
+        w_codes = [w_first[:], w_second[:], w_rest[:, 0:QUARTER], w_rest[:, QUARTER:HALF]]
+        scores = [psum.tile([P, PACK, QUARTER], F32, name="scores%d" % q) for q in range(4)]
+        for q in range(4):
+            for t in range(PACK):
+                rows = slice(t * P, (t + 1) * P)
                 nc.tensor.matmul_mx(
-                    out=bank[:, t - t0, :],
-                    lhsT=xT_codes[:, t * P : (t + 1) * P].bitcast(E4M3),
-                    lhsT_scale=xT_scale[:, t * P : (t + 1) * P],
-                    rhs=w_codes[h][:].bitcast(E4M3),
-                    rhs_scale=w_scale[:, h * HALF : (h + 1) * HALF],
+                    out=scores[q][:, t, :],
+                    lhsT=xT_codes[:, rows].bitcast(E4M3),
+                    lhsT_scale=xT_scale[:, rows],
+                    rhs=w_codes[q].bitcast(E4M3),
+                    rhs_scale=w_scale[:, quarters[q]],
                     start=True,
                     stop=True,
                 )
 
-        factor = keep.tile([P, PACK, N], F32, name="factor")
-        first, second = slice(0, HALF), slice(HALF, N)
-        nc.scalar.activation(out=factor[:, 1, :], in_=y_low[:, 1, :], func=ACT.Copy, scale=neg_wt[:, 0:1])
-        nc.scalar.activation(out=factor[:, 3, first], in_=y_high[0][:, 1, :], func=ACT.Copy, scale=neg_wt[:, 1:2])
-        for t, cols, src in (
-            (0, slice(0, N), y_low[:, 0, :]),
-            (2, first, y_high[0][:, 0, :]),
-            (2, second, y_high[1][:, 0, :]),
-            (3, second, y_high[1][:, 1, :]),
-        ):
+        factor = [keep.tile([P, PACK, HALF], F32, name="factor%d" % h, align_bytes=64) for h in range(2)]
+        for e in range(2):
+            t = 2 * e + 1
+            nc.scalar.activation(out=factor[0][:, t, :], in_=labels[0][:, t, :], func=ACT.Copy, scale=neg_wt[:, e : e + 1])
+        for h, t in ((0, 0), (0, 2), (1, 0), (1, 1), (1, 2), (1, 3)):
             nc.gpsimd.tensor_scalar(
-                out=factor[:, t, cols], in0=src, scalar1=wt_sb[:, t : t + 1], scalar2=-1.0, op0=ALU.mult, op1=ALU.mult
+                out=factor[h][:, t, :], in0=labels[h][:, t, :], scalar1=wt_sb[:, t : t + 1], scalar2=-1.0,
+                op0=ALU.mult, op1=ALU.mult,
             )
-        hinge = [keep.tile([P, PACK, HALF], F32, name="hinge%d" % h, tag="hinge%d" % h, align_bytes=64) for h in range(2)]
-        steps = banks
-        margins = {}
-        for h, t0, t1 in steps:
-            if (h, t1) == (1, 2):
-                margins[h, t0] = shared.tile([P, t1 - t0, HALF], F32, name="margin_last", align_bytes=64, offset=8192)
-            elif (h, t1) == (0, 4):
-                margins[h, t0] = shared.tile([P, t1 - t0, HALF], F32, name="margin_mid", align_bytes=64, offset=10240)
-            else:
-                margins[h, t0] = keep.tile([P, t1 - t0, HALF], F32, name="margin%d%d" % (h, t0), align_bytes=64)
+        margins = [
+            keep.tile([P, PACK, QUARTER], F32, name="margin0", align_bytes=64),
+            keep.tile([P, PACK, QUARTER], F32, name="margin1", align_bytes=64),
+            keep.tile([P, PACK, QUARTER], F32, name="margin2", align_bytes=64),
+            shared.tile([P, PACK, QUARTER], F32, name="margin3", align_bytes=64, offset=8192),
+        ]
+        hinge = [
+            keep.tile([P, PACK, QUARTER], F32, name="hinge0", align_bytes=64),
+            keep.tile([P, PACK, QUARTER], F32, name="hinge1", align_bytes=64),
+            shared.tile([P, PACK, QUARTER], F32, name="hinge2", align_bytes=64, offset=0),
+            shared.tile([P, PACK, QUARTER], F32, name="hinge3", align_bytes=64, offset=40960 - 1024),
+        ]
 
-        def make_margin(h, t0, t1):
-            bank, e = scores[h, t0]
-            nc.vector.tensor_tensor(
-                out=margins[h, t0][:], in0=bank[:, e : e + t1 - t0, :],
-                in1=y_low[:, :, h * HALF : (h + 1) * HALF] if t0 == 0 else y_high[h][:], op=ALU.mult,
+        def within_half(tiles, q):
+            return tiles[q // 2][:, :, quarters[q % 2]]
+
+        def make_hinge(q):
+            nc.scalar.activation(out=hinge[q][:], in_=margins[q][:], func=ACT.Relu, bias=1.0, scale=-1.0)
+
+        xm_bf_mid = shared.tile([P, 2, P * PACK], BF16, name="xm_bf_mid", align_bytes=64, offset=8192)
+        xm_bf = [
+            shared.tile([P, P * PACK], BF16, name="xm_bf0", align_bytes=64, offset=10240),
+            xm_bf_mid[:, 0, :],
+            xm_bf_mid[:, 1, :],
+            shared.tile([P, P * PACK], BF16, name="xm_bf3", align_bytes=64, offset=40960 - 512),
+        ]
+
+        def woven(k):
+            return (
+                xm_bf[k][:].rearrange("p (c i j) -> p c j i", i=4, j=PACK),
+                xm_raw[k].rearrange("p j (c i) -> p c j i", i=4),
             )
 
-        def make_hinge(h, t0, t1):
-            nc.scalar.activation(out=hinge[h][:, t0:t1, :], in_=margins[h, t0][:], func=ACT.Relu, bias=1.0, scale=-1.0)
+        def round_xm_on_scalar(k):
+            dst, src = woven(k)
+            nc.scalar.copy(out=dst, in_=src)
 
-        for step in steps[:2]:
-            make_margin(*step)
-            make_hinge(*step)
-        for step in steps[2:]:
-            make_margin(*step)
+        def round_xm_on_vector(k):
+            dst, src = woven(k)
+            nc.vector.tensor_copy(out=dst, in_=src)
 
-        xm_bf_first = shared.tile([P, P * PACK], BF16, name="xm_bf_first", align_bytes=64, offset=10240)
-        xm_bf_mid = shared.tile([P, 2, P * PACK], BF16, name="xm_bf_mid", align_bytes=64, offset=6400)
-        xm_bf = [xm_bf_first[:]] + [xm_bf_mid[:, k, :] for k in range(2)]
+        for q in range(4):
+            nc.vector.tensor_tensor(out=margins[q][:], in0=scores[q][:], in1=within_half(labels, q), op=ALU.mult)
+        make_hinge(0)
+        make_hinge(1)
+        round_xm_on_scalar(0)
+        make_hinge(2)
+        make_hinge(3)
+        nc.scalar.copy(
+            out=xm_bf_mid[:].rearrange("p k (c i j) -> p (k c) j i", i=4, j=PACK),
+            in_=xm_rest[:, :, 0 : 2 * P].rearrange("p j (c i) -> p c j i", i=4),
+        )
+
+        g_bf = [
+            keep.tile([P, HALF * PACK], BF16, name="g_bf0", align_bytes=64),
+            shared.tile([P, HALF * PACK], BF16, name="g_bf1", align_bytes=64, offset=10240),
+        ]
+        g_codes = keep.tile([P, N], U32, name="g_codes", align_bytes=64)
+        g_scale = keep.tile([P, N], U8, name="g_scale", align_bytes=64)
+        xm_codes = keep.tile([P, D], U32, name="xm_codes", align_bytes=64)
         xm_scale = keep.tile([P, D], U8, name="xm_scale", align_bytes=64)
-        g_bf = {}
 
-        def round_xm(k):
-            nc.scalar.copy(
-                out=xm_bf[k].rearrange("p (c i j) -> p c j i", i=4, j=PACK),
-                in_=xm_raw[k].rearrange("p j (c i) -> p c j i", i=4),
-            )
-
-        def make_g(h, tile):
-            g_bf[h] = tile
+        def make_g(q):
+            words = slice((q % 2) * QUARTER * PACK, (q % 2 + 1) * QUARTER * PACK)
             nc.vector.tensor_tensor(
-                out=g_bf[h][:].rearrange("p (c i t) -> p c t i", i=4, t=PACK),
-                in0=hinge[h][:].rearrange("p t (c i) -> p c t i", i=4),
-                in1=factor[:, :, h * HALF : (h + 1) * HALF].rearrange("p t (c i) -> p c t i", i=4),
+                out=g_bf[q // 2][:, words].rearrange("p (c i t) -> p c t i", i=4, t=PACK),
+                in0=hinge[q][:].rearrange("p t (c i) -> p c t i", i=4),
+                in1=within_half(factor, q).rearrange("p t (c i) -> p c t i", i=4),
                 op=ALU.mult,
             )
 
         def quantize_g(h):
-            cols = slice((h + 1) * HALF, (h + 2) * HALF)
-            nc.vector.quantize_mx(out=g_codes[:, cols].bitcast(E5M2), scales=g_scale[:, cols], in_=g_bf[h][:])
+            nc.vector.quantize_mx(
+                out=g_codes[:, halves[h]].bitcast(E5M2), scales=g_scale[:, halves[h]], in_=g_bf[h][:]
+            )
 
-        def gradient(k, first, keep_from, name):
+        def quantize_xm(k):
+            cols = slice(k * P, (k + 1) * P)
+            nc.vector.quantize_mx(out=xm_codes[:, cols].bitcast(E4M3), scales=xm_scale[:, cols], in_=xm_bf[k][:])
+
+        def gradient(k, slots):
             acc = psum_dw.tile([P, N], F32, name="acc")
             nc.tensor.matmul_mx(
-                out=acc[:],
+                out=acc[:, slots],
                 lhsT=xm_codes[:, k * P : (k + 1) * P].bitcast(E4M3),
                 lhsT_scale=xm_scale[:, k * P : (k + 1) * P],
-                rhs=g_codes[:, first : first + N].bitcast(E5M2),
-                rhs_scale=g_scale[:, first : first + N],
+                rhs=g_codes[:, slots].bitcast(E5M2),
+                rhs_scale=g_scale[:, slots],
                 start=True,
                 stop=True,
             )
-            dw = keep.tile([P, N - keep_from], F32, name=name, tag=name, align_bytes=64)
-            nc.scalar.copy(out=dw[:], in_=acc[:, keep_from:N])
-            return dw
+            return acc[:, slots]
 
-        round_xm(0)
-        for step in steps[2:]:
-            make_hinge(*step)
-        nc.scalar.copy(
-            out=xm_bf_mid[:].rearrange("p k (c i j) -> p (k c) j i", i=4, j=PACK),
-            in_=xm_rest[:].rearrange("p j (c i) -> p c j i", i=4),
-        )
-        make_g(0, keep.tile([P, HALF * PACK], BF16, name="g_bf0", align_bytes=64))
-        xm_codes = keep.tile([P, D], U32, name="xm_codes", tag="hinge0", align_bytes=64)
+        def scatter_on_scalar(k, h, values):
+            nc.scalar.activation(out=windows[k][:].indirect(listed(halves[h])), in_=values, func=ACT.Copy)
 
-        def quantize_xm(first, last, src):
-            cols = slice(first * P, last * P)
-            nc.vector.quantize_mx(out=xm_codes[:, cols].bitcast(E4M3), scales=xm_scale[:, cols], in_=src)
+        def store(k):
+            nc.sync.dma_start(out=out[k * P : (k + 1) * P, :], in_=windows[k][:])
 
-        quantize_xm(0, 1, xm_bf[0])
+        every = slice(0, N)
+        dw0 = [keep.tile([P, HALF], F32, name="dw0%d" % h, align_bytes=64) for h in range(2)]
+        dw2 = [keep.tile([P, HALF], F32, name="dw2%d" % h, align_bytes=64) for h in range(2)]
+        dw1 = keep.tile([P, N], F32, name="dw1", align_bytes=64)
+        dw3 = keep.tile([P, N], F32, name="dw3", align_bytes=64)
+
+        make_g(0)
+        make_g(1)
+        quantize_xm(0)
         quantize_g(0)
-        make_g(1, shared.tile([P, HALF * PACK], BF16, name="g_bf1", align_bytes=64, offset=10240))
-        quantize_xm(1, 3, xm_bf_mid[:].rearrange("p k c -> p (k c)"))
+        nc.scalar.copy(out=dw0[0][:], in_=gradient(0, halves[0]))
+        scatter_on_scalar(0, 0, dw0[0][:])
+        make_g(2)
+        make_g(3)
+        quantize_xm(1)
         quantize_g(1)
-        early = [gradient(k, 0, HALF, "dw_early%d" % k) for k in range(EARLY)]
-        xm_bf_last = shared.tile([P, P * PACK], BF16, name="xm_bf_last", align_bytes=64, offset=10240)
-        xm_bf.append(xm_bf_last[:])
-        round_xm(3)
-        quantize_xm(3, 4, xm_bf[3])
-        late = [gradient(k, HALF, HALF if k < EARLY else 0, "dw_late%d" % k) for k in range(D // P)]
-        for k in range(EARLY):
-            nc.vector.tensor_copy(windows[k][:].indirect(half_offsets[0]), early[k][:])
-        window = shared.tile([P, T], F32, name="window2", align_bytes=64, offset=8192)
-        nc.gpsimd.memset(window[:].bitcast(I32), 0)
-        windows.append(window)
-        for k in range(D // P):
-            window = windows[k % 3]
-            nc.vector.tensor_copy(window[:].indirect(half_offsets[1] if k < EARLY else offsets[:]), late[k][:])
-            pieces = (4, 2, 2, 1)[k]
-            for u in range(pieces):
-                cols = slice(u * T // pieces, (u + 1) * T // pieces)
-                nc.sync.dma_start(out=out[k * P : (k + 1) * P, cols], in_=window[:, cols])
+        quantize_xm(2)
+        round_xm_on_vector(3)
+        nc.vector.tensor_copy(out=dw0[1][:], in_=gradient(0, halves[1]))
+        scatter_on_scalar(0, 1, dw0[1][:])
+        store(0)
+        quantize_xm(3)
+        windows.append(shared.tile([P, T], F32, name="window2", align_bytes=64, offset=32768))
+        windows.append(shared.tile([P, T], F32, name="window3", align_bytes=64, offset=40960))
+        for k in (2, 3):
+            nc.gpsimd.memset(windows[k][:].bitcast(I32), 0)
+        nc.vector.tensor_copy(out=dw1[:], in_=gradient(1, every))
+        third = gradient(2, every)
+        nc.vector.tensor_copy(out=dw2[0][:], in_=third[:, halves[0]])
+        nc.vector.tensor_copy(windows[1][:].indirect(offsets[:]), dw1[:])
+        store(1)
+        nc.scalar.copy(out=dw2[1][:], in_=third[:, halves[1]])
+        for h in range(2):
+            scatter_on_scalar(2, h, dw2[h][:])
+        store(2)
+        nc.vector.tensor_copy(out=dw3[:], in_=gradient(3, every))
+        nc.vector.tensor_copy(windows[3][:].indirect(offsets[:]), dw3[:])
+        store(3)

@@ -39,7 +39,7 @@ def tile_attend_gsqh_w_kernel(tc, xT, w_words, w_scales, y, wt, xm, offs, out):
 
         table_scales = keep.tile([P, T // 4], I32, name="table_scales", align_bytes=64)
         nc.vector.memset(table_scales[:], 0)
-        windows = [keep.tile([P, T], F32, name="window%d" % k) for k in range(2)]
+        windows = [keep.tile([P, T], F32, name="window%d" % k) for k in range(3)]
         for window in windows:
             nc.vector.memset(window[:].bitcast(I32), 0)
 
@@ -109,7 +109,7 @@ def tile_attend_gsqh_w_kernel(tc, xT, w_words, w_scales, y, wt, xm, offs, out):
                 op0=ALU.mult, op1=ALU.mult,
             )
         margins = [
-            keep.tile([P, PACK, QUARTER], F32, name="margin0", align_bytes=64),
+            shared.tile([P, PACK, QUARTER], F32, name="margin0", align_bytes=64, offset=10240),
             keep.tile([P, PACK, QUARTER], F32, name="margin1", align_bytes=64),
             keep.tile([P, PACK, QUARTER], F32, name="margin2", align_bytes=64),
             shared.tile([P, PACK, QUARTER], F32, name="margin3", align_bytes=64, offset=8192),
@@ -229,10 +229,8 @@ def tile_attend_gsqh_w_kernel(tc, xT, w_words, w_scales, y, wt, xm, offs, out):
         scatter_on_scalar(0, 1, dw0[1][:])
         store(0)
         quantize_xm(3)
-        windows.append(shared.tile([P, T], F32, name="window2", align_bytes=64, offset=32768))
         windows.append(shared.tile([P, T], F32, name="window3", align_bytes=64, offset=40960))
-        for k in (2, 3):
-            nc.gpsimd.memset(windows[k][:].bitcast(I32), 0)
+        nc.gpsimd.memset(windows[3][:].bitcast(I32), 0)
         nc.vector.tensor_copy(out=dw1[:], in_=gradient(1, every))
         third = gradient(2, every)
         nc.vector.tensor_copy(out=dw2[0][:], in_=third[:, halves[0]])

@@ -47,8 +47,8 @@ def tile_attend_gsqh_w_kernel(tc, xT, w_words, w_scales, y, wt, xm, offs, out):
         nc.sync.dma_start(out=xT_raw[:], in_=xT[0].rearrange("(p j) r -> p j r", j=PACK))
         nc.sync.dma_start(offsets[:], offs)
         scale_rows = w_scales[0].bitcast(I32)
-        for q in range(4):
-            nc.sync.dma_start(out=table_scales[32 * q : 32 * q + 4, :], in_=scale_rows[4 * q : 4 * q + 4, :])
+        for i in range(4):
+            nc.sync.dma_start(out=table_scales[i:P:32, :], in_=scale_rows[i:16:4, :])
         table_words = keep.tile([P, T], I32, name="table_words", align_bytes=64)
         nc.sync.dma_start(out=table_words[:], in_=w_words[0].rearrange("p n j -> p (n j)").bitcast(I32))
         wt_sb = keep.tile([P, PACK], F32, name="wt_sb")
@@ -204,42 +204,46 @@ def tile_attend_gsqh_w_kernel(tc, xT, w_words, w_scales, y, wt, xm, offs, out):
         def scatter_on_scalar(k, h, values):
             nc.scalar.activation(out=windows[k][:].indirect(listed(halves[h])), in_=values, func=ACT.Copy)
 
+        def scatter_on_vector(k, slots, values):
+            nc.vector.tensor_copy(windows[k][:].indirect(listed(slots)), values)
+
         def store(k):
             nc.sync.dma_start(out=out[k * P : (k + 1) * P, :], in_=windows[k][:])
 
         every = slice(0, N)
-        dw0 = [keep.tile([P, HALF], F32, name="dw0%d" % h, align_bytes=64) for h in range(2)]
-        dw2 = [keep.tile([P, HALF], F32, name="dw2%d" % h, align_bytes=64) for h in range(2)]
-        dw1 = keep.tile([P, N], F32, name="dw1", align_bytes=64)
-        dw3 = keep.tile([P, N], F32, name="dw3", align_bytes=64)
+        dw = [keep.tile([P, N], F32, name="dw%d" % k, align_bytes=64) for k in range(4)]
 
         make_g(0)
         make_g(1)
         quantize_xm(0)
         quantize_g(0)
-        nc.scalar.copy(out=dw0[0][:], in_=gradient(0, halves[0]))
-        scatter_on_scalar(0, 0, dw0[0][:])
+        nc.scalar.copy(out=dw[0][:, halves[0]], in_=gradient(0, halves[0]))
+        scatter_on_scalar(0, 0, dw[0][:, halves[0]])
         make_g(2)
         make_g(3)
         quantize_xm(1)
         quantize_g(1)
         quantize_xm(2)
         round_xm_on_vector(3)
-        nc.vector.tensor_copy(out=dw0[1][:], in_=gradient(0, halves[1]))
-        scatter_on_scalar(0, 1, dw0[1][:])
-        store(0)
+        nc.vector.tensor_copy(out=dw[0][:, halves[1]], in_=gradient(0, halves[1]))
+        second = [gradient(1, halves[h]) for h in range(2)]
+        third = gradient(2, every)
         quantize_xm(3)
+        fourth = gradient(3, every)
         windows.append(shared.tile([P, T], F32, name="window3", align_bytes=64, offset=40960))
         nc.gpsimd.memset(windows[3][:].bitcast(I32), 0)
-        nc.vector.tensor_copy(out=dw1[:], in_=gradient(1, every))
-        third = gradient(2, every)
-        nc.vector.tensor_copy(out=dw2[0][:], in_=third[:, halves[0]])
-        nc.vector.tensor_copy(windows[1][:].indirect(offsets[:]), dw1[:])
+        scatter_on_vector(0, halves[1], dw[0][:, halves[1]])
+        store(0)
+        nc.scalar.copy(out=dw[1][:, halves[0]], in_=second[0])
+        scatter_on_scalar(1, 0, dw[1][:, halves[0]])
+        nc.scalar.copy(out=dw[2][:, halves[0]], in_=third[:, halves[0]])
+        nc.vector.tensor_copy(out=dw[1][:, halves[1]], in_=second[1])
+        nc.vector.tensor_copy(out=dw[2][:, halves[1]], in_=third[:, halves[1]])
+        nc.vector.tensor_copy(out=dw[3][:], in_=fourth)
+        scatter_on_scalar(1, 1, dw[1][:, halves[1]])
         store(1)
-        nc.scalar.copy(out=dw2[1][:], in_=third[:, halves[1]])
-        for h in range(2):
-            scatter_on_scalar(2, h, dw2[h][:])
+        scatter_on_vector(2, every, dw[2][:])
         store(2)
-        nc.vector.tensor_copy(out=dw3[:], in_=gradient(3, every))
-        nc.vector.tensor_copy(windows[3][:].indirect(offsets[:]), dw3[:])
+        for h in range(2):
+            scatter_on_scalar(3, h, dw[3][:, halves[h]])
         store(3)

@@ -62,7 +62,7 @@ def tile_attend_gsqh_w_kernel(tc, xT, w_words, w_scales, y, wt, xm, offs, out):
         nc.sync.dma_start(out=xm_first[:], in_=xm_rows[:, :, 0:P])
         xm_rest = shared.tile([P, PACK, D - P], F32, name="xm_rest", align_bytes=64, offset=24576)
         nc.sync.dma_start(out=xm_rest[:], in_=xm_rows[:, :, P:D])
-        xm_raw = [xm_first[:]] + [xm_rest[:, :, k * P : (k + 1) * P] for k in range(3)]
+        xm_raw = [xm_first[:]] + [xm_rest[:, :, 0:P]]
 
         xT_bf = shared.tile([P, R * PACK], BF16, name="xT_bf", align_bytes=64, offset=16384)
         xT_bf_by_row = xT_bf[:].rearrange("p (t m j) -> p m j t", t=PACK, j=PACK)
@@ -111,8 +111,8 @@ def tile_attend_gsqh_w_kernel(tc, xT, w_words, w_scales, y, wt, xm, offs, out):
         margins = [
             shared.tile([P, PACK, QUARTER], F32, name="margin0", align_bytes=64, offset=10240),
             keep.tile([P, PACK, QUARTER], F32, name="margin1", align_bytes=64),
-            keep.tile([P, PACK, QUARTER], F32, name="margin2", align_bytes=64),
-            shared.tile([P, PACK, QUARTER], F32, name="margin3", align_bytes=64, offset=8192),
+            shared.tile([P, PACK, QUARTER], F32, name="margin2", align_bytes=64, offset=8192),
+            keep.tile([P, PACK, QUARTER], F32, name="margin3", align_bytes=64),
         ]
         hinge = [
             keep.tile([P, PACK, QUARTER], F32, name="hinge0", align_bytes=64),
@@ -127,13 +127,11 @@ def tile_attend_gsqh_w_kernel(tc, xT, w_words, w_scales, y, wt, xm, offs, out):
         def make_hinge(q):
             nc.scalar.activation(out=hinge[q][:], in_=margins[q][:], func=ACT.Relu, bias=1.0, scale=-1.0)
 
-        xm_bf_mid = shared.tile([P, 2, P * PACK], BF16, name="xm_bf_mid", align_bytes=64, offset=8192)
         xm_bf = [
             shared.tile([P, P * PACK], BF16, name="xm_bf0", align_bytes=64, offset=10240),
-            xm_bf_mid[:, 0, :],
-            xm_bf_mid[:, 1, :],
-            shared.tile([P, P * PACK], BF16, name="xm_bf3", align_bytes=64, offset=40960 - 512),
+            shared.tile([P, P * PACK], BF16, name="xm_bf1", align_bytes=64, offset=8192),
         ]
+        xm_bf_last = shared.tile([P, 2 * P * PACK], BF16, name="xm_bf_last", align_bytes=64, offset=40960 - 512)
 
         def woven(k):
             return (
@@ -145,10 +143,6 @@ def tile_attend_gsqh_w_kernel(tc, xT, w_words, w_scales, y, wt, xm, offs, out):
             dst, src = woven(k)
             nc.scalar.copy(out=dst, in_=src)
 
-        def round_xm_on_vector(k):
-            dst, src = woven(k)
-            nc.vector.tensor_copy(out=dst, in_=src)
-
         for q in range(4):
             nc.vector.tensor_tensor(out=margins[q][:], in0=scores[q][:], in1=within_half(labels, q), op=ALU.mult)
         make_hinge(0)
@@ -156,10 +150,7 @@ def tile_attend_gsqh_w_kernel(tc, xT, w_words, w_scales, y, wt, xm, offs, out):
         round_xm_on_scalar(0)
         make_hinge(2)
         make_hinge(3)
-        nc.scalar.copy(
-            out=xm_bf_mid[:].rearrange("p k (c i j) -> p (k c) j i", i=4, j=PACK),
-            in_=xm_rest[:, :, 0 : 2 * P].rearrange("p j (c i) -> p c j i", i=4),
-        )
+        round_xm_on_scalar(1)
 
         g_bf = [
             keep.tile([P, HALF * PACK], BF16, name="g_bf0", align_bytes=64),
@@ -223,12 +214,16 @@ def tile_attend_gsqh_w_kernel(tc, xT, w_words, w_scales, y, wt, xm, offs, out):
         make_g(3)
         quantize_xm(1)
         quantize_g(1)
-        quantize_xm(2)
-        round_xm_on_vector(3)
+        nc.vector.tensor_copy(
+            out=xm_bf_last[:].rearrange("p (c i j) -> p c j i", i=4, j=PACK),
+            in_=xm_rest[:, :, P : 3 * P].rearrange("p j (c i) -> p c j i", i=4),
+        )
         nc.vector.tensor_copy(out=dw[0][:, halves[1]], in_=gradient(0, halves[1]))
         second = [gradient(1, halves[h]) for h in range(2)]
-        third = gradient(2, every)
-        quantize_xm(3)
+        nc.vector.quantize_mx(
+            out=xm_codes[:, 2 * P : D].bitcast(E4M3), scales=xm_scale[:, 2 * P : D], in_=xm_bf_last[:]
+        )
+        third = [gradient(2, halves[h]) for h in range(2)]
         fourth = gradient(3, every)
         windows.append(shared.tile([P, T], F32, name="window3", align_bytes=64, offset=40960))
         nc.gpsimd.memset(windows[3][:].bitcast(I32), 0)
@@ -236,14 +231,15 @@ def tile_attend_gsqh_w_kernel(tc, xT, w_words, w_scales, y, wt, xm, offs, out):
         store(0)
         nc.scalar.copy(out=dw[1][:, halves[0]], in_=second[0])
         scatter_on_scalar(1, 0, dw[1][:, halves[0]])
-        nc.scalar.copy(out=dw[2][:, halves[0]], in_=third[:, halves[0]])
+        nc.scalar.copy(out=dw[2][:, halves[0]], in_=third[0])
         nc.vector.tensor_copy(out=dw[1][:, halves[1]], in_=second[1])
-        nc.vector.tensor_copy(out=dw[2][:, halves[1]], in_=third[:, halves[1]])
-        nc.vector.tensor_copy(out=dw[3][:], in_=fourth)
+        nc.vector.tensor_copy(out=dw[2][:, halves[1]], in_=third[1])
+        nc.vector.tensor_copy(out=dw[3][:, halves[1]], in_=fourth[:, halves[1]])
         scatter_on_scalar(1, 1, dw[1][:, halves[1]])
         store(1)
+        nc.scalar.copy(out=dw[3][:, halves[0]], in_=fourth[:, halves[0]])
         scatter_on_vector(2, every, dw[2][:])
         store(2)
-        for h in range(2):
+        for h in (1, 0):
             scatter_on_scalar(3, h, dw[3][:, halves[h]])
         store(3)

@@ -28,7 +28,6 @@ def tile_attend_gsqh_w_kernel(tc, xT, w_words, w_scales, y, wt, xm, offs, out):
         keep = ctx.enter_context(tc.tile_pool(name="keep", bufs=1))
         shared = ctx.enter_context(tc.tile_pool(name="shared", bufs=1))
         psum = ctx.enter_context(tc.psum_pool(name="psum", bufs=1))
-        psum_dw = ctx.enter_context(tc.psum_pool(name="psum_dw", bufs=4))
 
         offsets = keep.tile([P, N // 16], U16, name="offsets")
         halves = [slice(h * HALF, (h + 1) * HALF) for h in range(2)]
@@ -60,9 +59,9 @@ def tile_attend_gsqh_w_kernel(tc, xT, w_words, w_scales, y, wt, xm, offs, out):
         xm_rows = xm[0].rearrange("(p j) d -> p j d", j=PACK)
         xm_first = shared.tile([P, PACK, P], F32, name="xm_first", align_bytes=64, offset=0)
         nc.sync.dma_start(out=xm_first[:], in_=xm_rows[:, :, 0:P])
-        xm_rest = shared.tile([P, PACK, D - P], F32, name="xm_rest", align_bytes=64, offset=24576)
+        xm_rest = keep.tile([P, PACK, D - P], F32, name="xm_rest", align_bytes=64)
         nc.sync.dma_start(out=xm_rest[:], in_=xm_rows[:, :, P:D])
-        xm_raw = [xm_first[:]] + [xm_rest[:, :, 0:P]]
+        xm_raw = [xm_first[:]] + [xm_rest[:, :, k * P : (k + 1) * P] for k in range(3)]
 
         xT_bf = shared.tile([P, R * PACK], BF16, name="xT_bf", align_bytes=64, offset=16384)
         xT_bf_by_row = xT_bf[:].rearrange("p (t m j) -> p m j t", t=PACK, j=PACK)
@@ -76,12 +75,14 @@ def tile_attend_gsqh_w_kernel(tc, xT, w_words, w_scales, y, wt, xm, offs, out):
         xT_scale = keep.tile([P, R], U8, name="xT_scale", align_bytes=64)
         nc.vector.quantize_mx(out=xT_codes[:].bitcast(E4M3), scales=xT_scale[:], in_=xT_bf[:])
 
-        neg_wt = keep.tile([P, 2], F32, name="neg_wt")
-        nc.scalar.activation(out=neg_wt[:], in_=wt_sb[:, 1:PACK:2], func=ACT.Copy, scale=-1.0)
+        neg_wt = keep.tile([P, PACK], F32, name="neg_wt")
+        nc.scalar.activation(out=neg_wt[:], in_=wt_sb[:], func=ACT.Copy, scale=-1.0)
+        windows.append(shared.tile([P, T], F32, name="window3", align_bytes=64, offset=16384 + 3072))
+        nc.gpsimd.memset(windows[3][:].bitcast(I32), 0)
 
-        w_first = shared.tile([P, QUARTER], U32, name="w_first", align_bytes=64, offset=16384)
-        w_second = shared.tile([P, QUARTER], U32, name="w_second", align_bytes=64, offset=16384 + 512)
-        w_rest = shared.tile([P, HALF], U32, name="w_rest", align_bytes=64, offset=16384 + 1024)
+        w_first = shared.tile([P, QUARTER], U32, name="w_first", align_bytes=64, offset=16384 + 512)
+        w_second = shared.tile([P, QUARTER], U32, name="w_second", align_bytes=64, offset=16384 + 1024)
+        w_rest = shared.tile([P, HALF], U32, name="w_rest", align_bytes=64, offset=16384 + 1536)
         for codes, slots in ((w_first, quarters[0]), (w_second, quarters[1]), (w_rest, halves[1])):
             nc.vector.tensor_copy(codes[:], table_words[:].bitcast(U32).indirect(listed(slots)))
         w_codes = [w_first[:], w_second[:], w_rest[:, 0:QUARTER], w_rest[:, QUARTER:HALF]]
@@ -99,13 +100,15 @@ def tile_attend_gsqh_w_kernel(tc, xT, w_words, w_scales, y, wt, xm, offs, out):
                     stop=True,
                 )
 
-        factor = [keep.tile([P, PACK, HALF], F32, name="factor%d" % h, align_bytes=64) for h in range(2)]
-        for e in range(2):
-            t = 2 * e + 1
-            nc.scalar.activation(out=factor[0][:, t, :], in_=labels[0][:, t, :], func=ACT.Copy, scale=neg_wt[:, e : e + 1])
-        for h, t in ((0, 0), (0, 2), (1, 0), (1, 1), (1, 2), (1, 3)):
+        factor = [
+            keep.tile([P, PACK, HALF], F32, name="factor0", align_bytes=64),
+            shared.tile([P, PACK, HALF], F32, name="factor1", align_bytes=64, offset=16384 + 512 - 4096),
+        ]
+        for t in range(PACK):
+            nc.scalar.activation(out=factor[0][:, t, :], in_=labels[0][:, t, :], func=ACT.Copy, scale=neg_wt[:, t : t + 1])
+        for t in range(PACK):
             nc.gpsimd.tensor_scalar(
-                out=factor[h][:, t, :], in0=labels[h][:, t, :], scalar1=wt_sb[:, t : t + 1], scalar2=-1.0,
+                out=factor[1][:, t, :], in0=labels[1][:, t, :], scalar1=wt_sb[:, t : t + 1], scalar2=-1.0,
                 op0=ALU.mult, op1=ALU.mult,
             )
         margins = [
@@ -130,8 +133,9 @@ def tile_attend_gsqh_w_kernel(tc, xT, w_words, w_scales, y, wt, xm, offs, out):
         xm_bf = [
             shared.tile([P, P * PACK], BF16, name="xm_bf0", align_bytes=64, offset=10240),
             shared.tile([P, P * PACK], BF16, name="xm_bf1", align_bytes=64, offset=8192),
+            shared.tile([P, P * PACK], BF16, name="xm_bf2", align_bytes=64, offset=40960 - 512),
+            shared.tile([P, P * PACK], BF16, name="xm_bf3", align_bytes=64, offset=40960 - 512),
         ]
-        xm_bf_last = shared.tile([P, 2 * P * PACK], BF16, name="xm_bf_last", align_bytes=64, offset=40960 - 512)
 
         def woven(k):
             return (
@@ -158,7 +162,12 @@ def tile_attend_gsqh_w_kernel(tc, xT, w_words, w_scales, y, wt, xm, offs, out):
         ]
         g_codes = keep.tile([P, N], U32, name="g_codes", align_bytes=64)
         g_scale = keep.tile([P, N], U8, name="g_scale", align_bytes=64)
-        xm_codes = keep.tile([P, D], U32, name="xm_codes", align_bytes=64)
+        xm_codes = [
+            keep.tile([P, P], U32, name="xm_codes0", align_bytes=64),
+            shared.tile([P, P], U32, name="xm_codes1", align_bytes=64, offset=40960 - 1024),
+            keep.tile([P, P], U32, name="xm_codes2", align_bytes=64),
+            keep.tile([P, P], U32, name="xm_codes3", align_bytes=64),
+        ]
         xm_scale = keep.tile([P, D], U8, name="xm_scale", align_bytes=64)
 
         def make_g(q):
@@ -170,20 +179,21 @@ def tile_attend_gsqh_w_kernel(tc, xT, w_words, w_scales, y, wt, xm, offs, out):
                 op=ALU.mult,
             )
 
-        def quantize_g(h):
+        def quantize_g(q):
+            words = slice((q % 2) * QUARTER * PACK, (q % 2 + 1) * QUARTER * PACK)
             nc.vector.quantize_mx(
-                out=g_codes[:, halves[h]].bitcast(E5M2), scales=g_scale[:, halves[h]], in_=g_bf[h][:]
+                out=g_codes[:, quarters[q]].bitcast(E5M2), scales=g_scale[:, quarters[q]], in_=g_bf[q // 2][:, words]
             )
 
         def quantize_xm(k):
             cols = slice(k * P, (k + 1) * P)
-            nc.vector.quantize_mx(out=xm_codes[:, cols].bitcast(E4M3), scales=xm_scale[:, cols], in_=xm_bf[k][:])
+            nc.vector.quantize_mx(out=xm_codes[k][:].bitcast(E4M3), scales=xm_scale[:, cols], in_=xm_bf[k][:])
 
-        def gradient(k, slots):
-            acc = psum_dw.tile([P, N], F32, name="acc")
+        def gradient(k, slots, bank):
+            acc = psum.tile([P, N], F32, name=bank)
             nc.tensor.matmul_mx(
                 out=acc[:, slots],
-                lhsT=xm_codes[:, k * P : (k + 1) * P].bitcast(E4M3),
+                lhsT=xm_codes[k][:].bitcast(E4M3),
                 lhsT_scale=xm_scale[:, k * P : (k + 1) * P],
                 rhs=g_codes[:, slots].bitcast(E5M2),
                 rhs_scale=g_scale[:, slots],
@@ -207,26 +217,28 @@ def tile_attend_gsqh_w_kernel(tc, xT, w_words, w_scales, y, wt, xm, offs, out):
         make_g(0)
         make_g(1)
         quantize_xm(0)
-        quantize_g(0)
-        nc.scalar.copy(out=dw[0][:, halves[0]], in_=gradient(0, halves[0]))
+        for q in (0, 1):
+            quantize_g(q)
+        for q in (0, 1):
+            nc.scalar.copy(out=dw[0][:, quarters[q]], in_=gradient(0, quarters[q], "acc%d" % q))
         scatter_on_scalar(0, 0, dw[0][:, halves[0]])
         make_g(2)
         make_g(3)
+        for q in (2, 3):
+            quantize_g(q)
+        first = [gradient(0, quarters[q], "acc%d" % q) for q in (2, 3)]
         quantize_xm(1)
-        quantize_g(1)
-        nc.vector.tensor_copy(
-            out=xm_bf_last[:].rearrange("p (c i j) -> p c j i", i=4, j=PACK),
-            in_=xm_rest[:, :, P : 3 * P].rearrange("p j (c i) -> p c j i", i=4),
+        second = [gradient(1, halves[h], "scores%d" % h) for h in range(2)]
+        dst, src = woven(2)
+        nc.vector.tensor_copy(out=dst, in_=src)
+        for q in (2, 3):
+            nc.vector.tensor_copy(out=dw[0][:, quarters[q]], in_=first[q - 2])
+        quantize_xm(2)
+        third = [gradient(2, halves[h], "scores%d" % (2 + h)) for h in range(2)]
+        nc.gpsimd.tensor_scalar(
+            out=xm_bf[3][:].rearrange("p (c j) -> p c j", j=PACK), in0=xm_raw[3].rearrange("p j c -> p c j"),
+            scalar1=1.0, scalar2=0.0, op0=ALU.mult, op1=ALU.add,
         )
-        nc.vector.tensor_copy(out=dw[0][:, halves[1]], in_=gradient(0, halves[1]))
-        second = [gradient(1, halves[h]) for h in range(2)]
-        nc.vector.quantize_mx(
-            out=xm_codes[:, 2 * P : D].bitcast(E4M3), scales=xm_scale[:, 2 * P : D], in_=xm_bf_last[:]
-        )
-        third = [gradient(2, halves[h]) for h in range(2)]
-        fourth = gradient(3, every)
-        windows.append(shared.tile([P, T], F32, name="window3", align_bytes=64, offset=40960))
-        nc.gpsimd.memset(windows[3][:].bitcast(I32), 0)
         scatter_on_vector(0, halves[1], dw[0][:, halves[1]])
         store(0)
         nc.scalar.copy(out=dw[1][:, halves[0]], in_=second[0])
@@ -234,12 +246,14 @@ def tile_attend_gsqh_w_kernel(tc, xT, w_words, w_scales, y, wt, xm, offs, out):
         nc.scalar.copy(out=dw[2][:, halves[0]], in_=third[0])
         nc.vector.tensor_copy(out=dw[1][:, halves[1]], in_=second[1])
         nc.vector.tensor_copy(out=dw[2][:, halves[1]], in_=third[1])
-        nc.vector.tensor_copy(out=dw[3][:, halves[1]], in_=fourth[:, halves[1]])
+        quantize_xm(3)
         scatter_on_scalar(1, 1, dw[1][:, halves[1]])
         store(1)
-        nc.scalar.copy(out=dw[3][:, halves[0]], in_=fourth[:, halves[0]])
         scatter_on_vector(2, every, dw[2][:])
         store(2)
-        for h in (1, 0):
+        fourth = gradient(3, every, "acc0")
+        for h in range(2):
+            nc.scalar.copy(out=dw[3][:, halves[h]], in_=fourth[:, halves[h]])
+        for h in range(2):
             scatter_on_scalar(3, h, dw[3][:, halves[h]])
         store(3)

@@ -117,18 +117,19 @@ def tile_attend_gsqh_w_kernel(tc, xT, w_words, w_scales, y, wt, xm, offs, out):
             shared.tile([P, PACK, QUARTER], F32, name="margin2", align_bytes=64, offset=8192),
             keep.tile([P, PACK, QUARTER], F32, name="margin3", align_bytes=64),
         ]
+        hinge_first = shared.tile([P, PACK, HALF], F32, name="hinge_first", align_bytes=64, offset=32768)
         hinge = [
-            keep.tile([P, PACK, QUARTER], F32, name="hinge0", align_bytes=64),
-            keep.tile([P, PACK, QUARTER], F32, name="hinge1", align_bytes=64),
-            shared.tile([P, PACK, QUARTER], F32, name="hinge2", align_bytes=64, offset=0),
-            shared.tile([P, PACK, QUARTER], F32, name="hinge3", align_bytes=64, offset=40960 - 1024),
+            hinge_first[:, :, quarters[0]],
+            hinge_first[:, :, quarters[1]],
+            shared.tile([P, PACK, QUARTER], F32, name="hinge2", align_bytes=64, offset=0)[:],
+            shared.tile([P, PACK, QUARTER], F32, name="hinge3", align_bytes=64, offset=40960 - 1024)[:],
         ]
 
         def within_half(tiles, q):
             return tiles[q // 2][:, :, quarters[q % 2]]
 
         def make_hinge(q):
-            nc.scalar.activation(out=hinge[q][:], in_=margins[q][:], func=ACT.Relu, bias=1.0, scale=-1.0)
+            nc.scalar.activation(out=hinge[q], in_=margins[q][:], func=ACT.Relu, bias=1.0, scale=-1.0)
 
         xm_bf = [
             shared.tile([P, P * PACK], BF16, name="xm_bf0", align_bytes=64, offset=10240),
@@ -158,7 +159,7 @@ def tile_attend_gsqh_w_kernel(tc, xT, w_words, w_scales, y, wt, xm, offs, out):
 
         g_bf = [
             keep.tile([P, HALF * PACK], BF16, name="g_bf0", align_bytes=64),
-            shared.tile([P, HALF * PACK], BF16, name="g_bf1", align_bytes=64, offset=10240),
+            shared.tile([P, HALF * PACK], BF16, name="g_bf1", align_bytes=64, offset=32768),
         ]
         g_codes = keep.tile([P, N], U32, name="g_codes", align_bytes=64)
         g_scale = keep.tile([P, N], U8, name="g_scale", align_bytes=64)
@@ -170,19 +171,20 @@ def tile_attend_gsqh_w_kernel(tc, xT, w_words, w_scales, y, wt, xm, offs, out):
         ]
         xm_scale = keep.tile([P, D], U8, name="xm_scale", align_bytes=64)
 
-        def make_g(q):
-            words = slice((q % 2) * QUARTER * PACK, (q % 2 + 1) * QUARTER * PACK)
+        def make_g(rounded, hinges, factors):
             nc.vector.tensor_tensor(
-                out=g_bf[q // 2][:, words].rearrange("p (c i t) -> p c t i", i=4, t=PACK),
-                in0=hinge[q][:].rearrange("p t (c i) -> p c t i", i=4),
-                in1=within_half(factor, q).rearrange("p t (c i) -> p c t i", i=4),
+                out=rounded.rearrange("p (c i t) -> p c t i", i=4, t=PACK),
+                in0=hinges.rearrange("p t (c i) -> p c t i", i=4),
+                in1=factors.rearrange("p t (c i) -> p c t i", i=4),
                 op=ALU.mult,
             )
 
+        def g_words(q):
+            return g_bf[q // 2][:, (q % 2) * QUARTER * PACK : (q % 2 + 1) * QUARTER * PACK]
+
         def quantize_g(q):
-            words = slice((q % 2) * QUARTER * PACK, (q % 2 + 1) * QUARTER * PACK)
             nc.vector.quantize_mx(
-                out=g_codes[:, quarters[q]].bitcast(E5M2), scales=g_scale[:, quarters[q]], in_=g_bf[q // 2][:, words]
+                out=g_codes[:, quarters[q]].bitcast(E5M2), scales=g_scale[:, quarters[q]], in_=g_words(q)
             )
 
         def quantize_xm(k):
@@ -214,16 +216,15 @@ def tile_attend_gsqh_w_kernel(tc, xT, w_words, w_scales, y, wt, xm, offs, out):
         every = slice(0, N)
         dw = [keep.tile([P, N], F32, name="dw%d" % k, align_bytes=64) for k in range(4)]
 
-        make_g(0)
-        make_g(1)
+        make_g(g_bf[0][:], hinge_first[:], factor[0][:])
         quantize_xm(0)
         for q in (0, 1):
             quantize_g(q)
         for q in (0, 1):
             nc.scalar.copy(out=dw[0][:, quarters[q]], in_=gradient(0, quarters[q], "acc%d" % q))
         scatter_on_scalar(0, 0, dw[0][:, halves[0]])
-        make_g(2)
-        make_g(3)
+        for q in (2, 3):
+            make_g(g_words(q), hinge[q], within_half(factor, q))
         for q in (2, 3):
             quantize_g(q)
         first = [gradient(0, quarters[q], "acc%d" % q) for q in (2, 3)]
@@ -234,7 +235,7 @@ def tile_attend_gsqh_w_kernel(tc, xT, w_words, w_scales, y, wt, xm, offs, out):
         for q in (2, 3):
             nc.vector.tensor_copy(out=dw[0][:, quarters[q]], in_=first[q - 2])
         quantize_xm(2)
-        third = [gradient(2, halves[h], "scores%d" % (2 + h)) for h in range(2)]
+        third = gradient(2, every, "scores2")
         nc.gpsimd.tensor_scalar(
             out=xm_bf[3][:].rearrange("p (c j) -> p c j", j=PACK), in0=xm_raw[3].rearrange("p j c -> p c j"),
             scalar1=1.0, scalar2=0.0, op0=ALU.mult, op1=ALU.add,
@@ -243,9 +244,8 @@ def tile_attend_gsqh_w_kernel(tc, xT, w_words, w_scales, y, wt, xm, offs, out):
         store(0)
         nc.scalar.copy(out=dw[1][:, halves[0]], in_=second[0])
         scatter_on_scalar(1, 0, dw[1][:, halves[0]])
-        nc.scalar.copy(out=dw[2][:, halves[0]], in_=third[0])
         nc.vector.tensor_copy(out=dw[1][:, halves[1]], in_=second[1])
-        nc.vector.tensor_copy(out=dw[2][:, halves[1]], in_=third[1])
+        nc.vector.tensor_copy(out=dw[2][:], in_=third)
         quantize_xm(3)
         scatter_on_scalar(1, 1, dw[1][:, halves[1]])
         store(1)

@@ -36,30 +36,30 @@ def tile_attend_gsqh_w_kernel(tc, xT, w_words, w_scales, y, wt, xm, offs, out):
         def listed(slots):
             return offsets[:, slots.start // 16 : slots.stop // 16]
 
-        table_scales = keep.tile([P, T // 4], I32, name="table_scales", align_bytes=64)
+        table_scales = keep.tile([P, T // 4], I32, name="table_scales", align_bytes=256)
         nc.vector.memset(table_scales[:], 0)
-        windows = [keep.tile([P, T], F32, name="window%d" % k) for k in range(3)]
+        windows = [keep.tile([P, T], F32, name="window%d" % k, align_bytes=256) for k in range(3)]
         for window in windows:
             nc.vector.memset(window[:].bitcast(I32), 0)
 
-        xT_raw = keep.tile([P, PACK, R], F32, name="xT_raw", align_bytes=64)
+        xT_raw = keep.tile([P, PACK, R], F32, name="xT_raw", align_bytes=256)
         nc.sync.dma_start(out=xT_raw[:], in_=xT[0].rearrange("(p j) r -> p j r", j=PACK))
         nc.sync.dma_start(offsets[:], offs)
         scale_rows = w_scales[0].bitcast(I32)
         for i in range(4):
             nc.sync.dma_start(out=table_scales[i:P:32, :], in_=scale_rows[i:16:4, :])
-        table_words = keep.tile([P, T], I32, name="table_words", align_bytes=64)
+        table_words = keep.tile([P, T], I32, name="table_words", align_bytes=256)
         nc.sync.dma_start(out=table_words[:], in_=w_words[0].rearrange("p n j -> p (n j)").bitcast(I32))
         wt_sb = keep.tile([P, PACK], F32, name="wt_sb")
         nc.sync.dma_start(out=wt_sb[:], in_=wt[0].rearrange("(p t) o -> p (t o)", t=PACK))
         y_rows = y[0].rearrange("(p t) n -> p t n", t=PACK)
-        labels = [keep.tile([P, PACK, HALF], F32, name="labels%d" % h, align_bytes=64) for h in range(2)]
+        labels = [keep.tile([P, PACK, HALF], F32, name="labels%d" % h, align_bytes=256) for h in range(2)]
         for h in range(2):
             nc.sync.dma_start(out=labels[h][:], in_=y_rows[:, :, halves[h]])
         xm_rows = xm[0].rearrange("(p j) d -> p j d", j=PACK)
-        xm_first = shared.tile([P, PACK, P], F32, name="xm_first", align_bytes=64, offset=0)
+        xm_first = shared.tile([P, PACK, P], F32, name="xm_first", align_bytes=256, offset=0)
         nc.sync.dma_start(out=xm_first[:], in_=xm_rows[:, :, 0:P])
-        xm_rest = keep.tile([P, PACK, D - P], F32, name="xm_rest", align_bytes=64)
+        xm_rest = keep.tile([P, PACK, D - P], F32, name="xm_rest", align_bytes=256)
         nc.sync.dma_start(out=xm_rest[:], in_=xm_rows[:, :, P:D])
         xm_raw = [xm_first[:]] + [xm_rest[:, :, k * P : (k + 1) * P] for k in range(3)]
 
@@ -77,7 +77,7 @@ def tile_attend_gsqh_w_kernel(tc, xT, w_words, w_scales, y, wt, xm, offs, out):
 
         neg_wt = keep.tile([P, PACK], F32, name="neg_wt")
         nc.scalar.activation(out=neg_wt[:], in_=wt_sb[:], func=ACT.Copy, scale=-1.0)
-        windows.append(shared.tile([P, T], F32, name="window3", align_bytes=64, offset=16384 + 3072))
+        windows.append(shared.tile([P, T], F32, name="window3", align_bytes=256, offset=16384 + 3072))
         nc.gpsimd.memset(windows[3][:].bitcast(I32), 0)
 
         w_first = shared.tile([P, QUARTER], U32, name="w_first", align_bytes=64, offset=16384 + 512)

@@ -42,6 +42,9 @@ def tile_attend_gsqh_w_kernel(tc, xT, w_words, w_scales, y, wt, xm, offs, out):
         for window in windows:
             nc.vector.memset(window[:].bitcast(I32), 0)
 
+        one = keep.tile([P, 1], F32, name="one")
+        nc.gpsimd.memset(one[:], 1.0)
+
         xT_raw = keep.tile([P, PACK, R], F32, name="xT_raw", align_bytes=256)
         nc.sync.dma_start(out=xT_raw[:], in_=xT[0].rearrange("(p j) r -> p j r", j=PACK))
         nc.sync.dma_start(offsets[:], offs)
@@ -61,7 +64,7 @@ def tile_attend_gsqh_w_kernel(tc, xT, w_words, w_scales, y, wt, xm, offs, out):
         nc.sync.dma_start(out=xm_first[:], in_=xm_rows[:, :, 0:P])
         xm_rest = keep.tile([P, PACK, D - P], F32, name="xm_rest", align_bytes=256)
         nc.sync.dma_start(out=xm_rest[:], in_=xm_rows[:, :, P:D])
-        xm_raw = [xm_first[:]] + [xm_rest[:, :, k * P : (k + 1) * P] for k in range(3)]
+        xm_raw = [xm_first[:]] + [xm_rest[:, :, 0:P], xm_rest[:, :, P : 3 * P]]
 
         xT_bf = shared.tile([P, R * PACK], BF16, name="xT_bf", align_bytes=64, offset=16384)
         xT_bf_by_row = xT_bf[:].rearrange("p (t m j) -> p m j t", t=PACK, j=PACK)
@@ -77,8 +80,6 @@ def tile_attend_gsqh_w_kernel(tc, xT, w_words, w_scales, y, wt, xm, offs, out):
 
         neg_wt = keep.tile([P, PACK], F32, name="neg_wt")
         nc.scalar.activation(out=neg_wt[:], in_=wt_sb[:], func=ACT.Copy, scale=-1.0)
-        windows.append(shared.tile([P, T], F32, name="window3", align_bytes=256, offset=16384 + 3072))
-        nc.gpsimd.memset(windows[3][:].bitcast(I32), 0)
 
         w_first = shared.tile([P, QUARTER], U32, name="w_first", align_bytes=64, offset=16384 + 512)
         w_second = shared.tile([P, QUARTER], U32, name="w_second", align_bytes=64, offset=16384 + 1024)
@@ -104,16 +105,16 @@ def tile_attend_gsqh_w_kernel(tc, xT, w_words, w_scales, y, wt, xm, offs, out):
             keep.tile([P, PACK, HALF], F32, name="factor0", align_bytes=64),
             shared.tile([P, PACK, HALF], F32, name="factor1", align_bytes=64, offset=16384 + 512 - 4096),
         ]
-        for t in range(PACK):
+        for t in range(2):
             nc.scalar.activation(out=factor[0][:, t, :], in_=labels[0][:, t, :], func=ACT.Copy, scale=neg_wt[:, t : t + 1])
-        for t in range(PACK):
+        for h, t in ((0, 2), (0, 3), (1, 0), (1, 1), (1, 2), (1, 3)):
             nc.gpsimd.tensor_scalar(
-                out=factor[1][:, t, :], in0=labels[1][:, t, :], scalar1=wt_sb[:, t : t + 1], scalar2=-1.0,
-                op0=ALU.mult, op1=ALU.mult,
+                out=factor[h][:, t, :], in0=labels[h][:, t, :], scalar1=neg_wt[:, t : t + 1], scalar2=0.0,
+                op0=ALU.mult, op1=ALU.add,
             )
         margins = [
-            shared.tile([P, PACK, QUARTER], F32, name="margin0", align_bytes=64, offset=10240),
-            keep.tile([P, PACK, QUARTER], F32, name="margin1", align_bytes=64),
+            keep.tile([P, PACK, QUARTER], F32, name="margin0", align_bytes=64),
+            shared.tile([P, PACK, QUARTER], F32, name="margin1", align_bytes=64, offset=10240),
             shared.tile([P, PACK, QUARTER], F32, name="margin2", align_bytes=64, offset=8192),
             keep.tile([P, PACK, QUARTER], F32, name="margin3", align_bytes=64),
         ]
@@ -121,7 +122,7 @@ def tile_attend_gsqh_w_kernel(tc, xT, w_words, w_scales, y, wt, xm, offs, out):
         hinge = [
             hinge_first[:, :, quarters[0]],
             hinge_first[:, :, quarters[1]],
-            shared.tile([P, PACK, QUARTER], F32, name="hinge2", align_bytes=64, offset=0)[:],
+            keep.tile([P, PACK, QUARTER], F32, name="hinge2", align_bytes=64)[:],
             shared.tile([P, PACK, QUARTER], F32, name="hinge3", align_bytes=64, offset=40960 - 1024)[:],
         ]
 
@@ -134,8 +135,7 @@ def tile_attend_gsqh_w_kernel(tc, xT, w_words, w_scales, y, wt, xm, offs, out):
         xm_bf = [
             shared.tile([P, P * PACK], BF16, name="xm_bf0", align_bytes=64, offset=10240),
             shared.tile([P, P * PACK], BF16, name="xm_bf1", align_bytes=64, offset=8192),
-            shared.tile([P, P * PACK], BF16, name="xm_bf2", align_bytes=64, offset=40960 - 512),
-            shared.tile([P, P * PACK], BF16, name="xm_bf3", align_bytes=64, offset=40960 - 512),
+            shared.tile([P, 2 * P * PACK], BF16, name="xm_bf2", align_bytes=64, offset=40960 - 512),
         ]
 
         def woven(k):
@@ -152,10 +152,11 @@ def tile_attend_gsqh_w_kernel(tc, xT, w_words, w_scales, y, wt, xm, offs, out):
             nc.vector.tensor_tensor(out=margins[q][:], in0=scores[q][:], in1=within_half(labels, q), op=ALU.mult)
         make_hinge(0)
         make_hinge(1)
-        round_xm_on_scalar(0)
         make_hinge(2)
+        round_xm_on_scalar(0)
         make_hinge(3)
-        round_xm_on_scalar(1)
+        dst1, src1 = woven(1)
+        nc.scalar.copy(out=dst1[:, 0:16], in_=src1[:, 0:16])
 
         g_bf = [
             keep.tile([P, HALF * PACK], BF16, name="g_bf0", align_bytes=64),
@@ -166,9 +167,10 @@ def tile_attend_gsqh_w_kernel(tc, xT, w_words, w_scales, y, wt, xm, offs, out):
         xm_codes = [
             keep.tile([P, P], U32, name="xm_codes0", align_bytes=64),
             shared.tile([P, P], U32, name="xm_codes1", align_bytes=64, offset=40960 - 1024),
-            keep.tile([P, P], U32, name="xm_codes2", align_bytes=64),
-            keep.tile([P, P], U32, name="xm_codes3", align_bytes=64),
+            keep.tile([P, 2 * P], U32, name="xm_codes2", align_bytes=64),
         ]
+        stationary = [xm_codes[0][:], xm_codes[1][:], xm_codes[2][:, 0:P], xm_codes[2][:, P : 2 * P]]
+        xm_cols = [slice(0, P), slice(P, 2 * P), slice(2 * P, D)]
         xm_scale = keep.tile([P, D], U8, name="xm_scale", align_bytes=64)
 
         def make_g(rounded, hinges, factors):
@@ -188,14 +190,13 @@ def tile_attend_gsqh_w_kernel(tc, xT, w_words, w_scales, y, wt, xm, offs, out):
             )
 
         def quantize_xm(k):
-            cols = slice(k * P, (k + 1) * P)
-            nc.vector.quantize_mx(out=xm_codes[k][:].bitcast(E4M3), scales=xm_scale[:, cols], in_=xm_bf[k][:])
+            nc.vector.quantize_mx(out=xm_codes[k][:].bitcast(E4M3), scales=xm_scale[:, xm_cols[k]], in_=xm_bf[k][:])
 
         def gradient(k, slots, bank):
             acc = psum.tile([P, N], F32, name=bank)
             nc.tensor.matmul_mx(
                 out=acc[:, slots],
-                lhsT=xm_codes[k][:].bitcast(E4M3),
+                lhsT=stationary[k].bitcast(E4M3),
                 lhsT_scale=xm_scale[:, k * P : (k + 1) * P],
                 rhs=g_codes[:, slots].bitcast(E5M2),
                 rhs_scale=g_scale[:, slots],
@@ -206,6 +207,9 @@ def tile_attend_gsqh_w_kernel(tc, xT, w_words, w_scales, y, wt, xm, offs, out):
 
         def scatter_on_scalar(k, h, values):
             nc.scalar.activation(out=windows[k][:].indirect(listed(halves[h])), in_=values, func=ACT.Copy)
+
+        def scatter_whole_on_scalar(k, values):
+            nc.scalar.activation(out=windows[k][:].indirect(offsets[:]), in_=values, func=ACT.Copy, scale=one[:])
 
         def scatter_on_vector(k, slots, values):
             nc.vector.tensor_copy(windows[k][:].indirect(listed(slots)), values)
@@ -222,6 +226,7 @@ def tile_attend_gsqh_w_kernel(tc, xT, w_words, w_scales, y, wt, xm, offs, out):
             quantize_g(q)
         for q in (0, 1):
             nc.scalar.copy(out=dw[0][:, quarters[q]], in_=gradient(0, quarters[q], "acc%d" % q))
+        nc.scalar.copy(out=dst1[:, 16:32], in_=src1[:, 16:32])
         scatter_on_scalar(0, 0, dw[0][:, halves[0]])
         for q in (2, 3):
             make_g(g_words(q), hinge[q], within_half(factor, q))
@@ -236,24 +241,19 @@ def tile_attend_gsqh_w_kernel(tc, xT, w_words, w_scales, y, wt, xm, offs, out):
             nc.vector.tensor_copy(out=dw[0][:, quarters[q]], in_=first[q - 2])
         quantize_xm(2)
         third = gradient(2, every, "scores2")
-        nc.gpsimd.tensor_scalar(
-            out=xm_bf[3][:].rearrange("p (c j) -> p c j", j=PACK), in0=xm_raw[3].rearrange("p j c -> p c j"),
-            scalar1=1.0, scalar2=0.0, op0=ALU.mult, op1=ALU.add,
-        )
+        fourth = gradient(3, every, "acc0")
+        windows.append(shared.tile([P, T], F32, name="window3", align_bytes=256, offset=40960 - 512))
+        nc.gpsimd.memset(windows[3][:].bitcast(I32), 0)
         scatter_on_vector(0, halves[1], dw[0][:, halves[1]])
         store(0)
-        nc.scalar.copy(out=dw[1][:, halves[0]], in_=second[0])
-        scatter_on_scalar(1, 0, dw[1][:, halves[0]])
-        nc.vector.tensor_copy(out=dw[1][:, halves[1]], in_=second[1])
-        nc.vector.tensor_copy(out=dw[2][:], in_=third)
-        quantize_xm(3)
-        scatter_on_scalar(1, 1, dw[1][:, halves[1]])
+        for h in range(2):
+            nc.scalar.copy(out=dw[1][:, halves[h]], in_=second[h])
+        scatter_whole_on_scalar(1, dw[1][:])
         store(1)
+        nc.vector.tensor_copy(out=dw[2][:], in_=third)
         scatter_on_vector(2, every, dw[2][:])
         store(2)
-        fourth = gradient(3, every, "acc0")
         for h in range(2):
             nc.scalar.copy(out=dw[3][:, halves[h]], in_=fourth[:, halves[h]])
-        for h in range(2):
-            scatter_on_scalar(3, h, dw[3][:, halves[h]])
+        scatter_whole_on_scalar(3, dw[3][:])
         store(3)

@@ -45,7 +45,7 @@ def tile_attend_gsqh_w_kernel(tc, xT, w_words, w_scales, y, wt, xm, offs, out):
         one = keep.tile([P, 1], F32, name="one")
         nc.gpsimd.memset(one[:], 1.0)
 
-        xT_raw = keep.tile([P, PACK, R], F32, name="xT_raw", align_bytes=256)
+        xT_raw = shared.tile([P, PACK, R], F32, name="xT_raw", align_bytes=256, offset=57344)
         nc.sync.dma_start(out=xT_raw[:], in_=xT[0].rearrange("(p j) r -> p j r", j=PACK))
         nc.sync.dma_start(offsets[:], offs)
         scale_rows = w_scales[0].bitcast(I32)
@@ -62,9 +62,9 @@ def tile_attend_gsqh_w_kernel(tc, xT, w_words, w_scales, y, wt, xm, offs, out):
         xm_rows = xm[0].rearrange("(p j) d -> p j d", j=PACK)
         xm_first = shared.tile([P, PACK, P], F32, name="xm_first", align_bytes=256, offset=0)
         nc.sync.dma_start(out=xm_first[:], in_=xm_rows[:, :, 0:P])
-        xm_rest = keep.tile([P, PACK, D - P], F32, name="xm_rest", align_bytes=256)
+        xm_rest = shared.tile([P, PACK, D - P], F32, name="xm_rest", align_bytes=256, offset=49152)
         nc.sync.dma_start(out=xm_rest[:], in_=xm_rows[:, :, P:D])
-        xm_raw = [xm_first[:]] + [xm_rest[:, :, 0:P], xm_rest[:, :, P : 3 * P]]
+        xm_raw = [xm_first[:]] + [xm_rest[:, :, k * P : (k + 1) * P] for k in range(3)]
 
         xT_bf = shared.tile([P, R * PACK], BF16, name="xT_bf", align_bytes=64, offset=16384)
         xT_bf_by_row = xT_bf[:].rearrange("p (t m j) -> p m j t", t=PACK, j=PACK)
@@ -78,21 +78,21 @@ def tile_attend_gsqh_w_kernel(tc, xT, w_words, w_scales, y, wt, xm, offs, out):
         xT_scale = keep.tile([P, R], U8, name="xT_scale", align_bytes=64)
         nc.vector.quantize_mx(out=xT_codes[:].bitcast(E4M3), scales=xT_scale[:], in_=xT_bf[:])
 
-        neg_wt = keep.tile([P, PACK], F32, name="neg_wt")
-        nc.scalar.activation(out=neg_wt[:], in_=wt_sb[:], func=ACT.Copy, scale=-1.0)
+        neg_early = keep.tile([P, 2], F32, name="neg_early")
+        nc.scalar.activation(out=neg_early[:], in_=wt_sb[:, 0:2], func=ACT.Copy, scale=-1.0)
 
-        w_first = shared.tile([P, QUARTER], U32, name="w_first", align_bytes=64, offset=16384 + 512)
-        w_second = shared.tile([P, QUARTER], U32, name="w_second", align_bytes=64, offset=16384 + 1024)
-        w_rest = shared.tile([P, HALF], U32, name="w_rest", align_bytes=64, offset=16384 + 1536)
+        w_first = shared.tile([P, QUARTER], U32, name="w_first", align_bytes=64, offset=57344)
+        w_second = shared.tile([P, QUARTER], U32, name="w_second", align_bytes=64, offset=57344 + 512)
+        w_rest = shared.tile([P, HALF], U32, name="w_rest", align_bytes=64, offset=57344 + 1024)
         for codes, slots in ((w_first, quarters[0]), (w_second, quarters[1]), (w_rest, halves[1])):
             nc.vector.tensor_copy(codes[:], table_words[:].bitcast(U32).indirect(listed(slots)))
         w_codes = [w_first[:], w_second[:], w_rest[:, 0:QUARTER], w_rest[:, QUARTER:HALF]]
-        scores = [psum.tile([P, PACK, QUARTER], F32, name="scores%d" % q) for q in range(4)]
+        scores = [psum.tile([P, 2, QUARTER], F32, name="scores%d" % b) for b in range(8)]
         for q in range(4):
             for t in range(PACK):
                 rows = slice(t * P, (t + 1) * P)
                 nc.tensor.matmul_mx(
-                    out=scores[q][:, t, :],
+                    out=scores[2 * q + t // 2][:, t % 2, :],
                     lhsT=xT_codes[:, rows].bitcast(E4M3),
                     lhsT_scale=xT_scale[:, rows],
                     rhs=w_codes[q].bitcast(E4M3),
@@ -106,16 +106,16 @@ def tile_attend_gsqh_w_kernel(tc, xT, w_words, w_scales, y, wt, xm, offs, out):
             shared.tile([P, PACK, HALF], F32, name="factor1", align_bytes=64, offset=16384 + 512 - 4096),
         ]
         for t in range(2):
-            nc.scalar.activation(out=factor[0][:, t, :], in_=labels[0][:, t, :], func=ACT.Copy, scale=neg_wt[:, t : t + 1])
-        for h, t in ((0, 2), (0, 3), (1, 0), (1, 1), (1, 2), (1, 3)):
+            nc.scalar.activation(out=factor[0][:, t, :], in_=labels[0][:, t, :], func=ACT.Copy, scale=neg_early[:, t : t + 1])
+        for h, t in ((0, 2), (0, 3), (1, 0), (1, 1)):
             nc.gpsimd.tensor_scalar(
-                out=factor[h][:, t, :], in0=labels[h][:, t, :], scalar1=neg_wt[:, t : t + 1], scalar2=0.0,
-                op0=ALU.mult, op1=ALU.add,
+                out=factor[h][:, t, :], in0=labels[h][:, t, :], scalar1=wt_sb[:, t : t + 1], scalar2=-1.0,
+                op0=ALU.mult, op1=ALU.mult,
             )
         margins = [
-            keep.tile([P, PACK, QUARTER], F32, name="margin0", align_bytes=64),
-            shared.tile([P, PACK, QUARTER], F32, name="margin1", align_bytes=64, offset=10240),
-            shared.tile([P, PACK, QUARTER], F32, name="margin2", align_bytes=64, offset=8192),
+            shared.tile([P, PACK, QUARTER], F32, name="margin0", align_bytes=64, offset=10240),
+            keep.tile([P, PACK, QUARTER], F32, name="margin1", align_bytes=64),
+            keep.tile([P, PACK, QUARTER], F32, name="margin2", align_bytes=64),
             keep.tile([P, PACK, QUARTER], F32, name="margin3", align_bytes=64),
         ]
         hinge_first = shared.tile([P, PACK, HALF], F32, name="hinge_first", align_bytes=64, offset=32768)
@@ -134,8 +134,9 @@ def tile_attend_gsqh_w_kernel(tc, xT, w_words, w_scales, y, wt, xm, offs, out):
 
         xm_bf = [
             shared.tile([P, P * PACK], BF16, name="xm_bf0", align_bytes=64, offset=10240),
-            shared.tile([P, P * PACK], BF16, name="xm_bf1", align_bytes=64, offset=8192),
-            shared.tile([P, 2 * P * PACK], BF16, name="xm_bf2", align_bytes=64, offset=40960 - 512),
+            shared.tile([P, P * PACK], BF16, name="xm_bf1", align_bytes=64, offset=32768 + 2048),
+            shared.tile([P, P * PACK], BF16, name="xm_bf2", align_bytes=64, offset=40960 - 512),
+            shared.tile([P, P * PACK], BF16, name="xm_bf3", align_bytes=64, offset=40960 - 512),
         ]
 
         def woven(k):
@@ -149,14 +150,20 @@ def tile_attend_gsqh_w_kernel(tc, xT, w_words, w_scales, y, wt, xm, offs, out):
             nc.scalar.copy(out=dst, in_=src)
 
         for q in range(4):
-            nc.vector.tensor_tensor(out=margins[q][:], in0=scores[q][:], in1=within_half(labels, q), op=ALU.mult)
+            for u in range(2):
+                pair = slice(2 * u, 2 * u + 2)
+                nc.vector.tensor_tensor(
+                    out=margins[q][:, pair, :], in0=scores[2 * q + u][:], in1=within_half(labels, q)[:, pair, :], op=ALU.mult
+                )
         make_hinge(0)
         make_hinge(1)
-        make_hinge(2)
+        neg_late = shared.tile([P, 2], F32, name="neg_late", align_bytes=64, offset=10240 + 1024)
+        nc.scalar.activation(out=neg_late[:], in_=wt_sb[:, 2:4], func=ACT.Copy, scale=-1.0)
         round_xm_on_scalar(0)
+        for t in (2, 3):
+            nc.scalar.activation(out=factor[1][:, t, :], in_=labels[1][:, t, :], func=ACT.Copy, scale=neg_late[:, t - 2 : t - 1])
+        make_hinge(2)
         make_hinge(3)
-        dst1, src1 = woven(1)
-        nc.scalar.copy(out=dst1[:, 0:16], in_=src1[:, 0:16])
 
         g_bf = [
             keep.tile([P, HALF * PACK], BF16, name="g_bf0", align_bytes=64),
@@ -166,11 +173,10 @@ def tile_attend_gsqh_w_kernel(tc, xT, w_words, w_scales, y, wt, xm, offs, out):
         g_scale = keep.tile([P, N], U8, name="g_scale", align_bytes=64)
         xm_codes = [
             keep.tile([P, P], U32, name="xm_codes0", align_bytes=64),
-            shared.tile([P, P], U32, name="xm_codes1", align_bytes=64, offset=40960 - 1024),
-            keep.tile([P, 2 * P], U32, name="xm_codes2", align_bytes=64),
+            keep.tile([P, P], U32, name="xm_codes1", align_bytes=64),
+            keep.tile([P, P], U32, name="xm_codes2", align_bytes=64),
+            keep.tile([P, P], U32, name="xm_codes3", align_bytes=64),
         ]
-        stationary = [xm_codes[0][:], xm_codes[1][:], xm_codes[2][:, 0:P], xm_codes[2][:, P : 2 * P]]
-        xm_cols = [slice(0, P), slice(P, 2 * P), slice(2 * P, D)]
         xm_scale = keep.tile([P, D], U8, name="xm_scale", align_bytes=64)
 
         def make_g(rounded, hinges, factors):
@@ -190,13 +196,14 @@ def tile_attend_gsqh_w_kernel(tc, xT, w_words, w_scales, y, wt, xm, offs, out):
             )
 
         def quantize_xm(k):
-            nc.vector.quantize_mx(out=xm_codes[k][:].bitcast(E4M3), scales=xm_scale[:, xm_cols[k]], in_=xm_bf[k][:])
+            cols = slice(k * P, (k + 1) * P)
+            nc.vector.quantize_mx(out=xm_codes[k][:].bitcast(E4M3), scales=xm_scale[:, cols], in_=xm_bf[k][:])
 
         def gradient(k, slots, bank):
             acc = psum.tile([P, N], F32, name=bank)
             nc.tensor.matmul_mx(
                 out=acc[:, slots],
-                lhsT=stationary[k].bitcast(E4M3),
+                lhsT=xm_codes[k][:].bitcast(E4M3),
                 lhsT_scale=xm_scale[:, k * P : (k + 1) * P],
                 rhs=g_codes[:, slots].bitcast(E5M2),
                 rhs_scale=g_scale[:, slots],
@@ -218,39 +225,51 @@ def tile_attend_gsqh_w_kernel(tc, xT, w_words, w_scales, y, wt, xm, offs, out):
             nc.sync.dma_start(out=out[k * P : (k + 1) * P, :], in_=windows[k][:])
 
         every = slice(0, N)
-        dw = [keep.tile([P, N], F32, name="dw%d" % k, align_bytes=64) for k in range(4)]
+        dw = [
+            keep.tile([P, N], F32, name="dw0", align_bytes=64),
+            keep.tile([P, N], F32, name="dw1", align_bytes=64),
+            shared.tile([P, N], F32, name="dw2", align_bytes=64, offset=49152),
+            keep.tile([P, N], F32, name="dw3", align_bytes=64),
+        ]
 
         make_g(g_bf[0][:], hinge_first[:], factor[0][:])
         quantize_xm(0)
         for q in (0, 1):
             quantize_g(q)
         for q in (0, 1):
-            nc.scalar.copy(out=dw[0][:, quarters[q]], in_=gradient(0, quarters[q], "acc%d" % q))
-        nc.scalar.copy(out=dst1[:, 16:32], in_=src1[:, 16:32])
+            nc.scalar.copy(out=dw[0][:, quarters[q]], in_=gradient(0, quarters[q], "scores%d" % q))
         scatter_on_scalar(0, 0, dw[0][:, halves[0]])
-        for q in (2, 3):
-            make_g(g_words(q), hinge[q], within_half(factor, q))
+        dst, src = woven(1)
+        nc.vector.tensor_copy(out=dst, in_=src)
+        make_g(g_words(2), hinge[2], within_half(factor, 2))
+        quantize_xm(1)
+        second = [gradient(1, halves[0], "scores4")]
+        make_g(g_words(3), hinge[3], within_half(factor, 3))
         for q in (2, 3):
             quantize_g(q)
-        first = [gradient(0, quarters[q], "acc%d" % q) for q in (2, 3)]
-        quantize_xm(1)
-        second = [gradient(1, halves[h], "scores%d" % h) for h in range(2)]
+        first = [gradient(0, quarters[q], "scores%d" % q) for q in (2, 3)]
+        second.append(gradient(1, halves[1], "scores5"))
         dst, src = woven(2)
         nc.vector.tensor_copy(out=dst, in_=src)
-        for q in (2, 3):
-            nc.vector.tensor_copy(out=dw[0][:, quarters[q]], in_=first[q - 2])
+        nc.vector.tensor_copy(out=dw[0][:, quarters[2]], in_=first[0])
+        nc.vector.tensor_copy(out=dw[0][:, quarters[3]], in_=first[1])
         quantize_xm(2)
-        third = gradient(2, every, "scores2")
-        fourth = gradient(3, every, "acc0")
-        windows.append(shared.tile([P, T], F32, name="window3", align_bytes=256, offset=40960 - 512))
-        nc.gpsimd.memset(windows[3][:].bitcast(I32), 0)
+        third = gradient(2, every, "scores6")
+        nc.gpsimd.tensor_scalar(
+            out=xm_bf[3][:].rearrange("p (c j) -> p c j", j=PACK), in0=xm_raw[3].rearrange("p j c -> p c j"),
+            scalar1=1.0, scalar2=0.0, op0=ALU.mult, op1=ALU.add,
+        )
         scatter_on_vector(0, halves[1], dw[0][:, halves[1]])
         store(0)
         for h in range(2):
             nc.scalar.copy(out=dw[1][:, halves[h]], in_=second[h])
         scatter_whole_on_scalar(1, dw[1][:])
         store(1)
+        quantize_xm(3)
         nc.vector.tensor_copy(out=dw[2][:], in_=third)
+        fourth = gradient(3, every, "scores7")
+        windows.append(shared.tile([P, T], F32, name="window3", align_bytes=256, offset=40960 - 512))
+        nc.gpsimd.memset(windows[3][:].bitcast(I32), 0)
         scatter_on_vector(2, every, dw[2][:])
         store(2)
         for h in range(2):

@@ -45,7 +45,7 @@ def tile_attend_gsqh_w_kernel(tc, xT, w_words, w_scales, y, wt, xm, offs, out):
         one = keep.tile([P, 1], F32, name="one")
         nc.gpsimd.memset(one[:], 1.0)
 
-        xT_raw = shared.tile([P, PACK, R], F32, name="xT_raw", align_bytes=256, offset=57344)
+        xT_raw = shared.tile([P, PACK, R], F32, name="xT_raw", align_bytes=256, offset=61440)
         nc.sync.dma_start(out=xT_raw[:], in_=xT[0].rearrange("(p j) r -> p j r", j=PACK))
         nc.sync.dma_start(offsets[:], offs)
         scale_rows = w_scales[0].bitcast(I32)
@@ -78,12 +78,12 @@ def tile_attend_gsqh_w_kernel(tc, xT, w_words, w_scales, y, wt, xm, offs, out):
         xT_scale = keep.tile([P, R], U8, name="xT_scale", align_bytes=64)
         nc.vector.quantize_mx(out=xT_codes[:].bitcast(E4M3), scales=xT_scale[:], in_=xT_bf[:])
 
-        neg_early = keep.tile([P, 2], F32, name="neg_early")
-        nc.scalar.activation(out=neg_early[:], in_=wt_sb[:, 0:2], func=ACT.Copy, scale=-1.0)
+        neg_wt = keep.tile([P, PACK], F32, name="neg_wt")
+        nc.scalar.activation(out=neg_wt[:], in_=wt_sb[:], func=ACT.Copy, scale=-1.0)
 
-        w_first = shared.tile([P, QUARTER], U32, name="w_first", align_bytes=64, offset=57344)
-        w_second = shared.tile([P, QUARTER], U32, name="w_second", align_bytes=64, offset=57344 + 512)
-        w_rest = shared.tile([P, HALF], U32, name="w_rest", align_bytes=64, offset=57344 + 1024)
+        w_first = shared.tile([P, QUARTER], U32, name="w_first", align_bytes=64, offset=61440)
+        w_second = shared.tile([P, QUARTER], U32, name="w_second", align_bytes=64, offset=61440 + 512)
+        w_rest = shared.tile([P, HALF], U32, name="w_rest", align_bytes=64, offset=61440 + 1024)
         for codes, slots in ((w_first, quarters[0]), (w_second, quarters[1]), (w_rest, halves[1])):
             nc.vector.tensor_copy(codes[:], table_words[:].bitcast(U32).indirect(listed(slots)))
         w_codes = [w_first[:], w_second[:], w_rest[:, 0:QUARTER], w_rest[:, QUARTER:HALF]]
@@ -103,10 +103,10 @@ def tile_attend_gsqh_w_kernel(tc, xT, w_words, w_scales, y, wt, xm, offs, out):
 
         factor = [
             keep.tile([P, PACK, HALF], F32, name="factor0", align_bytes=64),
-            shared.tile([P, PACK, HALF], F32, name="factor1", align_bytes=64, offset=16384 + 512 - 4096),
+            shared.tile([P, PACK, HALF], F32, name="factor1", align_bytes=64, offset=61440 + 1024 - 4096),
         ]
         for t in range(2):
-            nc.scalar.activation(out=factor[0][:, t, :], in_=labels[0][:, t, :], func=ACT.Copy, scale=neg_early[:, t : t + 1])
+            nc.scalar.activation(out=factor[0][:, t, :], in_=labels[0][:, t, :], func=ACT.Copy, scale=neg_wt[:, t : t + 1])
         for h, t in ((0, 2), (0, 3), (1, 0), (1, 1)):
             nc.gpsimd.tensor_scalar(
                 out=factor[h][:, t, :], in0=labels[h][:, t, :], scalar1=wt_sb[:, t : t + 1], scalar2=-1.0,
@@ -157,11 +157,9 @@ def tile_attend_gsqh_w_kernel(tc, xT, w_words, w_scales, y, wt, xm, offs, out):
                 )
         make_hinge(0)
         make_hinge(1)
-        neg_late = shared.tile([P, 2], F32, name="neg_late", align_bytes=64, offset=10240 + 1024)
-        nc.scalar.activation(out=neg_late[:], in_=wt_sb[:, 2:4], func=ACT.Copy, scale=-1.0)
+        nc.scalar.activation(out=factor[1][:, 2, :], in_=labels[1][:, 2, :], func=ACT.Copy, scale=neg_wt[:, 2:3])
         round_xm_on_scalar(0)
-        for t in (2, 3):
-            nc.scalar.activation(out=factor[1][:, t, :], in_=labels[1][:, t, :], func=ACT.Copy, scale=neg_late[:, t - 2 : t - 1])
+        nc.scalar.activation(out=factor[1][:, 3, :], in_=labels[1][:, 3, :], func=ACT.Copy, scale=neg_wt[:, 3:4])
         make_hinge(2)
         make_hinge(3)
 
@@ -238,17 +236,17 @@ def tile_attend_gsqh_w_kernel(tc, xT, w_words, w_scales, y, wt, xm, offs, out):
             quantize_g(q)
         for q in (0, 1):
             nc.scalar.copy(out=dw[0][:, quarters[q]], in_=gradient(0, quarters[q], "scores%d" % q))
-        scatter_on_scalar(0, 0, dw[0][:, halves[0]])
         dst, src = woven(1)
-        nc.vector.tensor_copy(out=dst, in_=src)
-        make_g(g_words(2), hinge[2], within_half(factor, 2))
-        quantize_xm(1)
-        second = [gradient(1, halves[0], "scores4")]
-        make_g(g_words(3), hinge[3], within_half(factor, 3))
+        nc.scalar.copy(out=dst[:, 16:32], in_=src[:, 16:32])
+        scatter_on_scalar(0, 0, dw[0][:, halves[0]])
+        nc.vector.tensor_copy(out=dst[:, 0:16], in_=src[:, 0:16])
         for q in (2, 3):
-            quantize_g(q)
+            make_g(g_words(q), hinge[q], within_half(factor, q))
+        quantize_g(2)
+        quantize_xm(1)
+        quantize_g(3)
         first = [gradient(0, quarters[q], "scores%d" % q) for q in (2, 3)]
-        second.append(gradient(1, halves[1], "scores5"))
+        second = [gradient(1, halves[h], "scores%d" % (4 + h)) for h in range(2)]
         dst, src = woven(2)
         nc.vector.tensor_copy(out=dst, in_=src)
         nc.vector.tensor_copy(out=dw[0][:, quarters[2]], in_=first[0])

from contextlib import ExitStack

import concourse.mybir as mybir

F32 = mybir.dt.float32
BF16 = mybir.dt.bfloat16
I32 = mybir.dt.int32
U32 = mybir.dt.uint32
U16 = mybir.dt.uint16
U8 = mybir.dt.uint8
E4M3 = mybir.dt.float8_e4m3fn_x4
E5M2 = mybir.dt.float8_e5m2_x4
ACT = mybir.ActivationFunctionType
ALU = mybir.AluOpType

P = 128
PACK = 4
N, T, D, R = 512, 2048, 512, 512
HALF = N // 2
QUARTER = N // 4
FLOPS = 2 * 2 * N * D * R
SPLIT = 48


def tile_attend_gsqh_w_kernel(tc, xT, w_words, w_scales, y, wt, xm, offs, out):
    nc = tc.nc
    with ExitStack() as ctx:
        keep = ctx.enter_context(tc.tile_pool(name="keep", bufs=1))
        shared = ctx.enter_context(tc.tile_pool(name="shared", bufs=1))
        psum = ctx.enter_context(tc.psum_pool(name="psum", bufs=1))

        offsets = keep.tile([P, N // 16], U16, name="offsets")
        halves = [slice(h * HALF, (h + 1) * HALF) for h in range(2)]
        quarters = [slice(q * QUARTER, (q + 1) * QUARTER) for q in range(4)]

        def listed(slots):
            return offsets[:, slots.start // 16 : slots.stop // 16]

        table_scales = keep.tile([P, T // 4], I32, name="table_scales", align_bytes=256)
        nc.vector.memset(table_scales[:], 0)
        windows = [keep.tile([P, T], F32, name="window%d" % k, align_bytes=256) for k in range(3)]
        for window in windows:
            nc.vector.memset(window[:].bitcast(I32), 0)

        one = keep.tile([P, 1], F32, name="one")
        nc.gpsimd.memset(one[:], 1.0)

        xT_raw = shared.tile([P, PACK, R], F32, name="xT_raw", align_bytes=256, offset=61440)
        nc.sync.dma_start(out=xT_raw[:], in_=xT[0].rearrange("(p j) r -> p j r", j=PACK))
        nc.sync.dma_start(offsets[:], offs)
        scale_rows = w_scales[0].bitcast(I32)
        for i in range(4):
            nc.sync.dma_start(out=table_scales[i:P:32, :], in_=scale_rows[i:16:4, :])
        table_words = keep.tile([P, T], I32, name="table_words", align_bytes=256)
        nc.sync.dma_start(out=table_words[:], in_=w_words[0].rearrange("p n j -> p (n j)").bitcast(I32))
        wt_sb = keep.tile([P, PACK], F32, name="wt_sb")
        nc.sync.dma_start(out=wt_sb[:], in_=wt[0].rearrange("(p t) o -> p (t o)", t=PACK))
        y_rows = y[0].rearrange("(p t) n -> p t n", t=PACK)
        labels = [keep.tile([P, PACK, HALF], F32, name="labels%d" % h, align_bytes=256) for h in range(2)]
        for h in range(2):
            nc.sync.dma_start(out=labels[h][:], in_=y_rows[:, :, halves[h]])
        xm_rows = xm[0].rearrange("(p j) d -> p j d", j=PACK)
        xm_first = shared.tile([P, PACK, P], F32, name="xm_first", align_bytes=256, offset=0)
        nc.sync.dma_start(out=xm_first[:], in_=xm_rows[:, :, 0:P])
        xm_rest = shared.tile([P, PACK, D - P], F32, name="xm_rest", align_bytes=256, offset=49152)
        nc.sync.dma_start(out=xm_rest[:], in_=xm_rows[:, :, P:D])
        xm_raw = [xm_first[:]] + [xm_rest[:, :, k * P : (k + 1) * P] for k in range(3)]

        xT_bf = shared.tile([P, R * PACK], BF16, name="xT_bf", align_bytes=64, offset=16384)
        xT_bf_by_row = xT_bf[:].rearrange("p (t m j) -> p m j t", t=PACK, j=PACK)
        xT_raw_by_row = xT_raw[:].rearrange("p j (m t) -> p m j t", t=PACK)
        nc.vector.tensor_copy(out=xT_bf_by_row[:, 0:SPLIT], in_=xT_raw_by_row[:, 0:SPLIT])
        nc.scalar.copy(out=xT_bf_by_row[:, SPLIT:P], in_=xT_raw_by_row[:, SPLIT:P])

        w_scale = keep.tile([P, N], U8, name="w_scale", align_bytes=64)
        nc.vector.tensor_copy(w_scale[:], table_scales[:].bitcast(U8).indirect(offsets[:]))
        xT_codes = keep.tile([P, R], U32, name="xT_codes", align_bytes=64)
        xT_scale = keep.tile([P, R], U8, name="xT_scale", align_bytes=64)
        nc.vector.quantize_mx(out=xT_codes[:].bitcast(E4M3), scales=xT_scale[:], in_=xT_bf[:])

        neg_wt = keep.tile([P, PACK], F32, name="neg_wt")
        nc.scalar.activation(out=neg_wt[:], in_=wt_sb[:], func=ACT.Copy, scale=-1.0)

        w_first = shared.tile([P, QUARTER], U32, name="w_first", align_bytes=64, offset=61440)
        w_second = shared.tile([P, QUARTER], U32, name="w_second", align_bytes=64, offset=61440 + 512)
        w_rest = shared.tile([P, HALF], U32, name="w_rest", align_bytes=64, offset=61440 + 1024)
        for codes, slots in ((w_first, quarters[0]), (w_second, quarters[1]), (w_rest, halves[1])):
            nc.vector.tensor_copy(codes[:], table_words[:].bitcast(U32).indirect(listed(slots)))
        w_codes = [w_first[:], w_second[:], w_rest[:, 0:QUARTER], w_rest[:, QUARTER:HALF]]
        scores = [psum.tile([P, 2, QUARTER], F32, name="scores%d" % b) for b in range(8)]
        for q in range(4):
            for t in range(PACK):
                rows = slice(t * P, (t + 1) * P)
                nc.tensor.matmul_mx(
                    out=scores[2 * q + t // 2][:, t % 2, :],
                    lhsT=xT_codes[:, rows].bitcast(E4M3),
                    lhsT_scale=xT_scale[:, rows],
                    rhs=w_codes[q].bitcast(E4M3),
                    rhs_scale=w_scale[:, quarters[q]],
                    start=True,
                    stop=True,
                )

        factor = [
            keep.tile([P, PACK, HALF], F32, name="factor0", align_bytes=64),
            shared.tile([P, PACK, HALF], F32, name="factor1", align_bytes=64, offset=61440 + 1024 - 4096),
        ]
        for t in range(2):
            nc.scalar.activation(out=factor[0][:, t, :], in_=labels[0][:, t, :], func=ACT.Copy, scale=neg_wt[:, t : t + 1])
        for h, t in ((0, 2), (0, 3), (1, 0), (1, 1)):
            nc.gpsimd.tensor_scalar(
                out=factor[h][:, t, :], in0=labels[h][:, t, :], scalar1=wt_sb[:, t : t + 1], scalar2=-1.0,
                op0=ALU.mult, op1=ALU.mult,
            )
        margins = [
            shared.tile([P, PACK, QUARTER], F32, name="margin0", align_bytes=64, offset=10240),
            keep.tile([P, PACK, QUARTER], F32, name="margin1", align_bytes=64),
            keep.tile([P, PACK, QUARTER], F32, name="margin2", align_bytes=64),
            keep.tile([P, PACK, QUARTER], F32, name="margin3", align_bytes=64),
        ]
        hinge_first = shared.tile([P, PACK, HALF], F32, name="hinge_first", align_bytes=64, offset=32768)
        hinge = [
            hinge_first[:, :, quarters[0]],
            hinge_first[:, :, quarters[1]],
            keep.tile([P, PACK, QUARTER], F32, name="hinge2", align_bytes=64)[:],
            shared.tile([P, PACK, QUARTER], F32, name="hinge3", align_bytes=64, offset=40960 - 1024)[:],
        ]

        def within_half(tiles, q):
            return tiles[q // 2][:, :, quarters[q % 2]]

        def make_hinge(q):
            nc.scalar.activation(out=hinge[q], in_=margins[q][:], func=ACT.Relu, bias=1.0, scale=-1.0)

        xm_bf = [
            shared.tile([P, P * PACK], BF16, name="xm_bf0", align_bytes=64, offset=10240),
            shared.tile([P, P * PACK], BF16, name="xm_bf1", align_bytes=64, offset=32768 + 2048),
            shared.tile([P, P * PACK], BF16, name="xm_bf2", align_bytes=64, offset=40960 - 512),
            shared.tile([P, P * PACK], BF16, name="xm_bf3", align_bytes=64, offset=40960 - 512),
        ]

        def woven(k):
            return (
                xm_bf[k][:].rearrange("p (c i j) -> p c j i", i=4, j=PACK),
                xm_raw[k].rearrange("p j (c i) -> p c j i", i=4),
            )

        def round_xm_on_scalar(k):
            dst, src = woven(k)
            nc.scalar.copy(out=dst, in_=src)

        for q in range(4):
            for u in range(2):
                pair = slice(2 * u, 2 * u + 2)
                nc.vector.tensor_tensor(
                    out=margins[q][:, pair, :], in0=scores[2 * q + u][:], in1=within_half(labels, q)[:, pair, :], op=ALU.mult
                )
        make_hinge(0)
        make_hinge(1)
        nc.scalar.activation(out=factor[1][:, 2, :], in_=labels[1][:, 2, :], func=ACT.Copy, scale=neg_wt[:, 2:3])
        round_xm_on_scalar(0)
        nc.scalar.activation(out=factor[1][:, 3, :], in_=labels[1][:, 3, :], func=ACT.Copy, scale=neg_wt[:, 3:4])
        make_hinge(2)
        make_hinge(3)

        g_bf = [
            keep.tile([P, HALF * PACK], BF16, name="g_bf0", align_bytes=64),
            shared.tile([P, HALF * PACK], BF16, name="g_bf1", align_bytes=64, offset=32768),
        ]
        g_codes = keep.tile([P, N], U32, name="g_codes", align_bytes=64)
        g_scale = keep.tile([P, N], U8, name="g_scale", align_bytes=64)
        xm_codes = [
            keep.tile([P, P], U32, name="xm_codes0", align_bytes=64),
            keep.tile([P, P], U32, name="xm_codes1", align_bytes=64),
            keep.tile([P, P], U32, name="xm_codes2", align_bytes=64),
            keep.tile([P, P], U32, name="xm_codes3", align_bytes=64),
        ]
        xm_scale = keep.tile([P, D], U8, name="xm_scale", align_bytes=64)

        def make_g(rounded, hinges, factors):
            nc.vector.tensor_tensor(
                out=rounded.rearrange("p (c i t) -> p c t i", i=4, t=PACK),
                in0=hinges.rearrange("p t (c i) -> p c t i", i=4),
                in1=factors.rearrange("p t (c i) -> p c t i", i=4),
                op=ALU.mult,
            )

        def g_words(q):
            return g_bf[q // 2][:, (q % 2) * QUARTER * PACK : (q % 2 + 1) * QUARTER * PACK]

        def quantize_g(q):
            nc.vector.quantize_mx(
                out=g_codes[:, quarters[q]].bitcast(E5M2), scales=g_scale[:, quarters[q]], in_=g_words(q)
            )

        def quantize_xm(k):
            cols = slice(k * P, (k + 1) * P)
            nc.vector.quantize_mx(out=xm_codes[k][:].bitcast(E4M3), scales=xm_scale[:, cols], in_=xm_bf[k][:])

        def gradient(k, slots, bank):
            acc = psum.tile([P, N], F32, name=bank)
            nc.tensor.matmul_mx(
                out=acc[:, slots],
                lhsT=xm_codes[k][:].bitcast(E4M3),
                lhsT_scale=xm_scale[:, k * P : (k + 1) * P],
                rhs=g_codes[:, slots].bitcast(E5M2),
                rhs_scale=g_scale[:, slots],
                start=True,
                stop=True,
            )
            return acc[:, slots]

        def scatter_on_scalar(k, h, values):
            nc.scalar.activation(out=windows[k][:].indirect(listed(halves[h])), in_=values, func=ACT.Copy)

        def scatter_whole_on_scalar(k, values):
            nc.scalar.activation(out=windows[k][:].indirect(offsets[:]), in_=values, func=ACT.Copy, scale=one[:])

        def scatter_on_vector(k, slots, values):
            nc.vector.tensor_copy(windows[k][:].indirect(listed(slots)), values)

        def store(k):
            nc.sync.dma_start(out=out[k * P : (k + 1) * P, :], in_=windows[k][:])

        every = slice(0, N)
        dw = [
            keep.tile([P, N], F32, name="dw0", align_bytes=64),
            keep.tile([P, N], F32, name="dw1", align_bytes=64),
            shared.tile([P, N], F32, name="dw2", align_bytes=64, offset=49152),
            keep.tile([P, N], F32, name="dw3", align_bytes=64),
        ]

        make_g(g_bf[0][:], hinge_first[:], factor[0][:])
        quantize_xm(0)
        for q in (0, 1):
            quantize_g(q)
        for q in (0, 1):
            nc.scalar.copy(out=dw[0][:, quarters[q]], in_=gradient(0, quarters[q], "scores%d" % q))
        dst, src = woven(1)
        nc.scalar.copy(out=dst[:, 16:32], in_=src[:, 16:32])
        scatter_on_scalar(0, 0, dw[0][:, halves[0]])
        nc.vector.tensor_copy(out=dst[:, 0:16], in_=src[:, 0:16])
        for q in (2, 3):
            make_g(g_words(q), hinge[q], within_half(factor, q))
        quantize_g(2)
        quantize_xm(1)
        quantize_g(3)
        first = [gradient(0, quarters[q], "scores%d" % q) for q in (2, 3)]
        second = [gradient(1, halves[h], "scores%d" % (4 + h)) for h in range(2)]
        dst, src = woven(2)
        nc.vector.tensor_copy(out=dst, in_=src)
        nc.vector.tensor_copy(out=dw[0][:, quarters[2]], in_=first[0])
        nc.vector.tensor_copy(out=dw[0][:, quarters[3]], in_=first[1])
        quantize_xm(2)
        third = gradient(2, every, "scores6")
        nc.gpsimd.tensor_scalar(
            out=xm_bf[3][:].rearrange("p (c j) -> p c j", j=PACK), in0=xm_raw[3].rearrange("p j c -> p c j"),
            scalar1=1.0, scalar2=0.0, op0=ALU.mult, op1=ALU.add,
        )
        scatter_on_vector(0, halves[1], dw[0][:, halves[1]])
        store(0)
        for h in range(2):
            nc.scalar.copy(out=dw[1][:, halves[h]], in_=second[h])
        scatter_whole_on_scalar(1, dw[1][:])
        store(1)
        quantize_xm(3)
        nc.vector.tensor_copy(out=dw[2][:], in_=third)
        fourth = gradient(3, every, "scores7")
        windows.append(shared.tile([P, T], F32, name="window3", align_bytes=256, offset=40960 - 512))
        nc.gpsimd.memset(windows[3][:].bitcast(I32), 0)
        scatter_on_vector(2, every, dw[2][:])
        store(2)
        for h in range(2):
            nc.scalar.copy(out=dw[3][:, halves[h]], in_=fourth[:, halves[h]])
        scatter_whole_on_scalar(3, dw[3][:])
        store(3)
